import numpy as np
import ml_dtypes


def mxq(x, axis, fmt="e4m3"):
    dtype, down = {"e4m3": (ml_dtypes.float8_e4m3fn, 7), "e5m2": (ml_dtypes.float8_e5m2, 14)}[fmt]
    v = np.moveaxis(np.asarray(x, np.float32).astype(ml_dtypes.bfloat16).astype(np.float64), axis, -1)
    blocks = v.reshape(v.shape[:-1] + (-1, 32))
    amax = np.abs(blocks).max(-1, keepdims=True)
    byte = np.maximum(np.where(amax > 0, np.frexp(amax)[1] - 1 + 127, 0) - down, 1)
    scale = np.exp2(byte - 127.0)
    codes = (blocks / scale).astype(np.float32).astype(dtype).astype(np.float64)
    return np.moveaxis((codes * scale).reshape(v.shape), -1, axis)


WIDE = False


def mx_kscale(k, group=512):
    if not WIDE:
        return np.ones(k)
    levels = np.array([18, -18])
    if group != 512:
        return np.exp2(np.random.permutation(np.resize(levels, k // group))).repeat(group)
    if k % 512:
        return np.exp2(np.random.permutation(np.resize(levels, k // 32))).repeat(32)
    a = np.empty((k // 512, 16))
    for p in range(k // 512):
        a[p, :8] = np.random.permutation(np.resize(levels, 8))
        for g in range(8):
            far = levels[np.abs(levels - a[p, g]) >= 10]
            a[p, g + 8] = far[np.random.randint(len(far))]
    return np.exp2(a.ravel()).repeat(32)


def f64(x):
    return np.asarray(x).astype(np.float64)


def gelu(v):
    return 0.5 * v * (1.0 + np.tanh(0.7978845608028654 * (v + 0.044715 * v ** 3)))


G, D, M, N, L = 4, 128, 128, 512, 1024


def setup_inputs():
    n = np.random.standard_normal
    s_d = mx_kscale(D, 0)
    return {
        "x": (n((G, D, L)) * s_d[:, None]).astype(np.float32),
        "w0": (n((G, D, M)) / np.sqrt(5 * D) / s_d[:, None]).astype(np.float32),
        "w1": (n((G, D, M)) / np.sqrt(5 * D) / s_d[:, None]).astype(np.float32),
        "w2": (n((G, D, M)) / np.sqrt(5 * D) / s_d[:, None]).astype(np.float32),
        "w3": (n((G, D, M)) / np.sqrt(5 * D) / s_d[:, None]).astype(np.float32),
        "w4": (n((G, D, M)) / np.sqrt(5 * D) / s_d[:, None]).astype(np.float32),
        "r": (n((G, M, N))).astype(np.float32),
    }


def reference(x, w0, w1, w2, w3, w4, r):
    w0q = mxq(f64(w0), 1, "e4m3")
    xq = mxq(f64(x), 1, "e4m3")
    w1q = mxq(f64(w1), 1, "e4m3")
    w2q = mxq(f64(w2), 1, "e4m3")
    w3q = mxq(f64(w3), 1, "e4m3")
    w4q = mxq(f64(w4), 1, "e4m3")
    z = (w0q.transpose(0, 2, 1) @ xq[..., :512]) + (w1q.transpose(0, 2, 1) @ xq[..., 128 : 640]) + (w2q.transpose(0, 2, 1) @ xq[..., 256 : 768]) + (w3q.transpose(0, 2, 1) @ xq[..., 384 : 896]) + (w4q.transpose(0, 2, 1) @ xq[..., 512 : 1024])
    y = gelu(z) + f64(r)
    return y

@@ -1,0 +1,103 @@
+from contextlib import ExitStack
+
+import concourse.mybir as mybir
+
+G, D, M, N, L = 4, 128, 128, 512, 1024
+TAPS = 5
+DILATION = 128
+FLOPS = 2 * G * TAPS * D * M * N
+
+F32 = mybir.dt.float32
+BF16 = mybir.dt.bfloat16
+U32 = mybir.dt.uint32
+U8 = mybir.dt.uint8
+FP8X4 = mybir.dt.float8_e4m3fn_x4
+GELU = mybir.ActivationFunctionType.Gelu_apprx_tanh
+
+P = 128
+PACK = 4
+ROWS = D // PACK
+
+
+def tile_rows_conv_res_kernel(tc, x, w0, w1, w2, w3, w4, r, out):
+    nc = tc.nc
+    weights = [w0, w1, w2, w3, w4]
+
+    with ExitStack() as ctx:
+        sb = ctx.enter_context(tc.tile_pool(name="sb", bufs=1))
+        psum = ctx.enter_context(tc.psum_pool(name="psum", bufs=1))
+        ctx.enter_context(tc.manual_schedule())
+
+        x_codes = sb.tile([P, L], U32, name="x_codes", align_bytes=64)
+        x_scales = sb.tile([P, L], U8, name="x_scales", align_bytes=64)
+        w_codes = [sb.tile([P, M], U32, name="w_codes%d" % t, align_bytes=64) for t in range(TAPS)]
+        w_scales = [sb.tile([P, M], U8, name="w_scales%d" % t, align_bytes=64) for t in range(TAPS)]
+        acc = [psum.tile([M, N], F32, name="acc%d" % g) for g in range(G)]
+
+        x_rows = x.rearrange("g (p j) l -> (g p) j l", j=PACK)
+
+        def x_piece(lo, hi, share):
+            return ("x%d" % lo, x_rows[:, :, lo:hi], x_codes[:, lo:hi], x_scales[:, lo:hi], share)
+
+        def w_piece(t, share):
+            rows = weights[t].rearrange("g (p j) m -> (g p) j m", j=PACK)
+            return ("w%d" % t, rows, w_codes[t][:], w_scales[t][:], share)
+
+        pieces = [
+            (x_piece(0, 512, 320), None),
+            (w_piece(0, 48), 0),
+            (x_piece(512, 768, 160), None),
+            (w_piece(1, 48), 1),
+            (w_piece(2, 48), 2),
+            (x_piece(768, 1024, 160), None),
+            (w_piece(3, 48), 3),
+            (w_piece(4, 48), 4),
+        ]
+
+        raws = []
+        for (name, rows, codes, scales, share), tap in pieces:
+            raw = sb.tile([P, PACK, rows.shape[2]], F32, name="raw_" + name)
+            nc.sync.dma_start(out=raw[:], in_=rows)
+            raws.append(raw)
+        res = []
+        for g in range(G):
+            res_g = sb.tile([M, N], F32, name="res%d" % g)
+            nc.sync.dma_start(out=res_g[:], in_=r[g])
+            res.append(res_g)
+
+        zero = sb.tile([P, 8], F32, name="zero")
+        bias = sb.tile([P, 8], F32, name="bias")
+        nc.vector.memset(zero[:], 0.0)
+        nc.scalar.activation(out=bias[:], in_=zero[:], func=GELU)
+
+        for raw, ((name, rows, codes, scales, share), tap) in zip(raws, pieces):
+            width = rows.shape[2]
+            grouped = sb.tile([P, width, PACK], BF16, name="grouped_" + name, align_bytes=64)
+            cols = raw[:].rearrange("p j w -> p w j")
+            nc.scalar.copy(out=grouped[:, share:, :], in_=cols[:, share:, :])
+            nc.vector.tensor_copy(out=grouped[:, :share, :], in_=cols[:, :share, :])
+            nc.vector.quantize_mx(
+                out=codes.bitcast(FP8X4),
+                scales=scales,
+                in_=grouped[:].rearrange("p w j -> p (w j)"),
+            )
+            if tap is not None:
+                window = slice(tap * DILATION, tap * DILATION + N)
+                for g in range(G):
+                    part = slice(g * ROWS, (g + 1) * ROWS)
+                    nc.tensor.matmul_mx(
+                        out=acc[g][:],
+                        lhsT=w_codes[tap][part, :].bitcast(FP8X4),
+                        lhsT_scale=w_scales[tap][part, :],
+                        rhs=x_codes[part, window].bitcast(FP8X4),
+                        rhs_scale=x_scales[part, window],
+                        start=(tap == 0),
+                        stop=(tap == TAPS - 1),
+                    )
+
+        for g, lo, hi in [(0, 0, 256), (0, 256, 512), (1, 0, 512), (2, 0, 512), (3, 0, 256), (3, 256, 512)]:
+            act = sb.tile([M, hi - lo], F32, name="act%d_%d" % (g, lo))
+            y = sb.tile([M, hi - lo], F32, name="y%d_%d" % (g, lo))
+            nc.scalar.activation(out=act[:], in_=acc[g][:, lo:hi], func=GELU, bias=bias[:, 0:1])
+            nc.vector.tensor_add(out=y[:], in0=act[:], in1=res[g][:, lo:hi])
+            nc.sync.dma_start(out=out[g, :, lo:hi], in_=y[:])

@@ -4,7 +4,8 @@ import concourse.mybir as mybir
 
 G, D, M, N, L = 4, 128, 128, 512, 1024
 TAPS = 5
-DILATION = 128
+STEP = 128
+BLOCKS = N // STEP
 FLOPS = 2 * G * TAPS * D * M * N
 
 F32 = mybir.dt.float32
@@ -17,87 +18,127 @@ GELU = mybir.ActivationFunctionType.Gelu_apprx_tanh
 P = 128
 PACK = 4
 ROWS = D // PACK
+VECTOR_SHARE = 48
 
 
 def tile_rows_conv_res_kernel(tc, x, w0, w1, w2, w3, w4, r, out):
     nc = tc.nc
-    weights = [w0, w1, w2, w3, w4]
 
     with ExitStack() as ctx:
         sb = ctx.enter_context(tc.tile_pool(name="sb", bufs=1))
         psum = ctx.enter_context(tc.psum_pool(name="psum", bufs=1))
         ctx.enter_context(tc.manual_schedule())
 
-        x_codes = sb.tile([P, L], U32, name="x_codes", align_bytes=64)
-        x_scales = sb.tile([P, L], U8, name="x_scales", align_bytes=64)
-        w_codes = [sb.tile([P, M], U32, name="w_codes%d" % t, align_bytes=64) for t in range(TAPS)]
-        w_scales = [sb.tile([P, M], U8, name="w_scales%d" % t, align_bytes=64) for t in range(TAPS)]
-        acc = [psum.tile([M, N], F32, name="acc%d" % g) for g in range(G)]
+        banks = [[psum.tile([M, 512], F32, name="bank%d_%d" % (g, s)) for s in range(2)] for g in range(G)]
 
         x_rows = x.rearrange("g (p j) l -> (g p) j l", j=PACK)
+        w_rows = [w.rearrange("g (p j) m -> (g p) j m", j=PACK) for w in (w0, w1, w2, w3, w4)]
+        r_rows = r.rearrange("g m n -> m g n")
+        out_rows = out.rearrange("g m n -> m g n")
 
-        def x_piece(lo, hi, share):
-            return ("x%d" % lo, x_rows[:, :, lo:hi], x_codes[:, lo:hi], x_scales[:, lo:hi], share)
+        def load(name, rows):
+            tile = sb.tile(list(rows.shape), F32, name=name)
+            nc.sync.dma_start(out=tile[:], in_=rows)
+            return tile
 
-        def w_piece(t, share):
-            rows = weights[t].rearrange("g (p j) m -> (g p) j m", j=PACK)
-            return ("w%d" % t, rows, w_codes[t][:], w_scales[t][:], share)
+        raw = {}
+        raw["w", 0] = load("raw_w0", w_rows[0])[:]
+        raw["x", 0] = load("raw_x0", x_rows[:, :, 0:STEP])[:]
+        for t in range(1, TAPS):
+            raw["x", t] = load("raw_x%d" % t, x_rows[:, :, t * STEP : (t + 1) * STEP])[:]
+            raw["w", t] = load("raw_w%d" % t, w_rows[t])[:]
+        raw["x", 5] = load("raw_x5", x_rows[:, :, 5 * STEP : 6 * STEP])[:]
+        last = load("raw_x67", x_rows[:, :, 6 * STEP : 8 * STEP])
+        raw["x", 6] = last[:, :, 0:STEP]
+        raw["x", 7] = last[:, :, STEP : 2 * STEP]
 
-        pieces = [
-            (x_piece(0, 512, 320), None),
-            (w_piece(0, 48), 0),
-            (x_piece(512, 768, 160), None),
-            (w_piece(1, 48), 1),
-            (w_piece(2, 48), 2),
-            (x_piece(768, 1024, 160), None),
-            (w_piece(3, 48), 3),
-            (w_piece(4, 48), 4),
-        ]
-
-        raws = []
-        for (name, rows, codes, scales, share), tap in pieces:
-            raw = sb.tile([P, PACK, rows.shape[2]], F32, name="raw_" + name)
-            nc.sync.dma_start(out=raw[:], in_=rows)
-            raws.append(raw)
-        res = []
-        for g in range(G):
-            res_g = sb.tile([M, N], F32, name="res%d" % g)
-            nc.sync.dma_start(out=res_g[:], in_=r[g])
-            res.append(res_g)
+        res = sb.tile([M, G, N], F32, name="res")
+        for gs, cs in [
+            (slice(0, 2), slice(0, 256)),
+            (slice(2, 4), slice(0, 256)),
+            (slice(0, 4), slice(256, 384)),
+            (slice(0, 4), slice(384, 512)),
+        ]:
+            nc.sync.dma_start(out=res[:, gs, cs], in_=r_rows[:, gs, cs])
 
         zero = sb.tile([P, 8], F32, name="zero")
         bias = sb.tile([P, 8], F32, name="bias")
         nc.vector.memset(zero[:], 0.0)
         nc.scalar.activation(out=bias[:], in_=zero[:], func=GELU)
 
-        for raw, ((name, rows, codes, scales, share), tap) in zip(raws, pieces):
-            width = rows.shape[2]
-            grouped = sb.tile([P, width, PACK], BF16, name="grouped_" + name, align_bytes=64)
-            cols = raw[:].rearrange("p j w -> p w j")
-            nc.scalar.copy(out=grouped[:, share:, :], in_=cols[:, share:, :])
-            nc.vector.tensor_copy(out=grouped[:, :share, :], in_=cols[:, :share, :])
-            nc.vector.quantize_mx(
-                out=codes.bitcast(FP8X4),
-                scales=scales,
-                in_=grouped[:].rearrange("p w j -> p (w j)"),
-            )
-            if tap is not None:
-                window = slice(tap * DILATION, tap * DILATION + N)
-                for g in range(G):
-                    part = slice(g * ROWS, (g + 1) * ROWS)
-                    nc.tensor.matmul_mx(
-                        out=acc[g][:],
-                        lhsT=w_codes[tap][part, :].bitcast(FP8X4),
-                        lhsT_scale=w_scales[tap][part, :],
-                        rhs=x_codes[part, window].bitcast(FP8X4),
-                        rhs_scale=x_scales[part, window],
-                        start=(tap == 0),
-                        stop=(tap == TAPS - 1),
-                    )
+        grouped, codes, scales = {}, {}, {}
 
-        for g, lo, hi in [(0, 0, 256), (0, 256, 512), (1, 0, 512), (2, 0, 512), (3, 0, 256), (3, 256, 512)]:
-            act = sb.tile([M, hi - lo], F32, name="act%d_%d" % (g, lo))
-            y = sb.tile([M, hi - lo], F32, name="y%d_%d" % (g, lo))
-            nc.scalar.activation(out=act[:], in_=acc[g][:, lo:hi], func=GELU, bias=bias[:, 0:1])
-            nc.vector.tensor_add(out=y[:], in0=act[:], in1=res[g][:, lo:hi])
-            nc.sync.dma_start(out=out[g, :, lo:hi], in_=y[:])
+        def interleave(key, share):
+            grouped[key] = sb.tile([P, STEP, PACK], BF16, name="grouped_%s%d" % key, align_bytes=64)
+            cols = raw[key].rearrange("p j w -> p w j")
+            if share < STEP:
+                nc.scalar.copy(out=grouped[key][:, share:, :], in_=cols[:, share:, :])
+            nc.vector.tensor_copy(out=grouped[key][:, :share, :], in_=cols[:, :share, :])
+
+        def quantize(key):
+            codes[key] = sb.tile([P, STEP], U32, name="codes_%s%d" % key, align_bytes=64)
+            scales[key] = sb.tile([P, STEP], U8, name="scales_%s%d" % key, align_bytes=64)
+            nc.vector.quantize_mx(
+                out=codes[key][:].bitcast(FP8X4),
+                scales=scales[key][:],
+                in_=grouped[key][:].rearrange("p w j -> p (w j)"),
+            )
+
+        def prepare(key):
+            interleave(key, VECTOR_SHARE)
+            quantize(key)
+
+        def multiply(b, t):
+            for g in range(G):
+                part = slice(g * ROWS, (g + 1) * ROWS)
+                nc.tensor.matmul_mx(
+                    out=banks[g][b % 2][:, 0:STEP],
+                    lhsT=codes["w", t][part, :].bitcast(FP8X4),
+                    lhsT_scale=scales["w", t][part, :],
+                    rhs=codes["x", b + t][part, :].bitcast(FP8X4),
+                    rhs_scale=scales["x", b + t][part, :],
+                    start=(t == 0),
+                    stop=(t == TAPS - 1),
+                )
+
+        act = sb.tile([M, G, N], F32, name="act")
+        y = sb.tile([M, G, N], F32, name="y")
+
+        def gelu(b):
+            for g in range(G):
+                nc.scalar.activation(
+                    out=act[:, g, b * STEP : (b + 1) * STEP],
+                    in_=banks[g][b % 2][:, 0:STEP],
+                    func=GELU,
+                    bias=bias[:, 0:1],
+                )
+
+        def finish(gs, cs):
+            nc.vector.tensor_add(out=y[:, gs, cs], in0=act[:, gs, cs], in1=res[:, gs, cs])
+            nc.sync.dma_start(out=out_rows[:, gs, cs], in_=y[:, gs, cs])
+
+        prepare(("w", 0))
+        prepare(("x", 0))
+        multiply(0, 0)
+        for t in range(1, TAPS):
+            prepare(("x", t))
+            multiply(1, t - 1)
+            prepare(("w", t))
+            multiply(0, t)
+        prepare(("x", 5))
+        multiply(1, TAPS - 1)
+        gelu(0)
+        gelu(1)
+        interleave(("x", 6), STEP)
+        interleave(("x", 7), STEP)
+        quantize(("x", 6))
+        quantize(("x", 7))
+        for b in (2, 3):
+            for t in range(TAPS):
+                multiply(b, t)
+            gelu(b)
+        finish(slice(0, 2), slice(0, 256))
+        finish(slice(2, 4), slice(0, 256))
+        finish(slice(0, 4), slice(256, 384))
+        finish(slice(0, 2), slice(384, 512))
+        finish(slice(2, 4), slice(384, 512))

@@ -18,7 +18,7 @@ GELU = mybir.ActivationFunctionType.Gelu_apprx_tanh
 P = 128
 PACK = 4
 ROWS = D // PACK
-VECTOR_SHARE = 48
+HALF = N // 2
 
 
 def tile_rows_conv_res_kernel(tc, x, w0, w1, w2, w3, w4, r, out):
@@ -41,25 +41,29 @@ def tile_rows_conv_res_kernel(tc, x, w0, w1, w2, w3, w4, r, out):
             nc.sync.dma_start(out=tile[:], in_=rows)
             return tile
 
+        pairs = [
+            (("x", 0), ("x", 1)),
+            (("x", 2), ("w", 1)),
+            (("x", 3), ("w", 2)),
+            (("x", 4), ("w", 3)),
+            (("w", 4), ("x", 5)),
+            (("x", 6), ("x", 7)),
+        ]
         raw = {}
         raw["w", 0] = load("raw_w0", w_rows[0])[:]
-        raw["x", 0] = load("raw_x0", x_rows[:, :, 0:STEP])[:]
-        for t in range(1, TAPS):
-            raw["x", t] = load("raw_x%d" % t, x_rows[:, :, t * STEP : (t + 1) * STEP])[:]
-            raw["w", t] = load("raw_w%d" % t, w_rows[t])[:]
-        raw["x", 5] = load("raw_x5", x_rows[:, :, 5 * STEP : 6 * STEP])[:]
-        last = load("raw_x67", x_rows[:, :, 6 * STEP : 8 * STEP])
-        raw["x", 6] = last[:, :, 0:STEP]
-        raw["x", 7] = last[:, :, STEP : 2 * STEP]
+        first = load("raw_x01", x_rows[:, :, 0 : 2 * STEP])
+        raw["x", 0] = first[:, :, 0:STEP]
+        raw["x", 1] = first[:, :, STEP : 2 * STEP]
+        for pair in pairs[1:]:
+            for kind, i in pair:
+                rows = w_rows[i] if kind == "w" else x_rows[:, :, i * STEP : (i + 1) * STEP]
+                raw[kind, i] = load("raw_%s%d" % (kind, i), rows)[:]
 
         res = sb.tile([M, G, N], F32, name="res")
-        for gs, cs in [
-            (slice(0, 2), slice(0, 256)),
-            (slice(2, 4), slice(0, 256)),
-            (slice(0, 4), slice(256, 384)),
-            (slice(0, 4), slice(384, 512)),
-        ]:
-            nc.sync.dma_start(out=res[:, gs, cs], in_=r_rows[:, gs, cs])
+        for h in range(2):
+            for gs in (slice(0, 2), slice(2, 4)):
+                cs = slice(h * HALF, (h + 1) * HALF)
+                nc.sync.dma_start(out=res[:, gs, cs], in_=r_rows[:, gs, cs])
 
         zero = sb.tile([P, 8], F32, name="zero")
         bias = sb.tile([P, 8], F32, name="bias")
@@ -68,12 +72,9 @@ def tile_rows_conv_res_kernel(tc, x, w0, w1, w2, w3, w4, r, out):
 
         grouped, codes, scales = {}, {}, {}
 
-        def interleave(key, share):
+        def interleave(key, copy):
             grouped[key] = sb.tile([P, STEP, PACK], BF16, name="grouped_%s%d" % key, align_bytes=64)
-            cols = raw[key].rearrange("p j w -> p w j")
-            if share < STEP:
-                nc.scalar.copy(out=grouped[key][:, share:, :], in_=cols[:, share:, :])
-            nc.vector.tensor_copy(out=grouped[key][:, :share, :], in_=cols[:, :share, :])
+            copy(out=grouped[key][:], in_=raw[key].rearrange("p j w -> p w j"))
 
         def quantize(key):
             codes[key] = sb.tile([P, STEP], U32, name="codes_%s%d" % key, align_bytes=64)
@@ -84,61 +85,47 @@ def tile_rows_conv_res_kernel(tc, x, w0, w1, w2, w3, w4, r, out):
                 in_=grouped[key][:].rearrange("p w j -> p (w j)"),
             )
 
-        def prepare(key):
-            interleave(key, VECTOR_SHARE)
-            quantize(key)
-
         def multiply(b, t):
             for g in range(G):
                 part = slice(g * ROWS, (g + 1) * ROWS)
                 nc.tensor.matmul_mx(
-                    out=banks[g][b % 2][:, 0:STEP],
+                    out=banks[g][b // 2][:, (b % 2) * STEP : (b % 2 + 1) * STEP],
                     lhsT=codes["w", t][part, :].bitcast(FP8X4),
                     lhsT_scale=scales["w", t][part, :],
                     rhs=codes["x", b + t][part, :].bitcast(FP8X4),
                     rhs_scale=scales["x", b + t][part, :],
-                    start=(t == 0),
-                    stop=(t == TAPS - 1),
+                    start=(t == 0 and b % 2 == 0),
+                    stop=(t == TAPS - 1 and b % 2 == 1),
                 )
 
         act = sb.tile([M, G, N], F32, name="act")
         y = sb.tile([M, G, N], F32, name="y")
 
-        def gelu(b):
-            for g in range(G):
-                nc.scalar.activation(
-                    out=act[:, g, b * STEP : (b + 1) * STEP],
-                    in_=banks[g][b % 2][:, 0:STEP],
-                    func=GELU,
-                    bias=bias[:, 0:1],
-                )
-
-        def finish(gs, cs):
+        def finish(h, gs):
+            cs = slice(h * HALF, (h + 1) * HALF)
+            for g in range(gs.start, gs.stop):
+                nc.scalar.activation(out=act[:, g, cs], in_=banks[g][h][:, 0:HALF], func=GELU, bias=bias[:, 0:1])
             nc.vector.tensor_add(out=y[:, gs, cs], in0=act[:, gs, cs], in1=res[:, gs, cs])
             nc.sync.dma_start(out=out_rows[:, gs, cs], in_=y[:, gs, cs])
 
-        prepare(("w", 0))
-        prepare(("x", 0))
-        multiply(0, 0)
-        for t in range(1, TAPS):
-            prepare(("x", t))
-            multiply(1, t - 1)
-            prepare(("w", t))
-            multiply(0, t)
-        prepare(("x", 5))
-        multiply(1, TAPS - 1)
-        gelu(0)
-        gelu(1)
-        interleave(("x", 6), STEP)
-        interleave(("x", 7), STEP)
-        quantize(("x", 6))
-        quantize(("x", 7))
-        for b in (2, 3):
-            for t in range(TAPS):
+        interleave(("w", 0), nc.vector.tensor_copy)
+        quantize(("w", 0))
+        todo = [(b, t) for b in range(BLOCKS) for t in range(TAPS)]
+        for early, late in pairs:
+            interleave(early, nc.scalar.copy)
+            interleave(late, nc.vector.tensor_copy)
+            quantize(early)
+            quantize(late)
+            ready = [(b, t) for b, t in todo if ("w", t) in codes and ("x", b + t) in codes]
+            for b, t in ready:
                 multiply(b, t)
-            gelu(b)
-        finish(slice(0, 2), slice(0, 256))
-        finish(slice(2, 4), slice(0, 256))
-        finish(slice(0, 4), slice(256, 384))
-        finish(slice(0, 2), slice(384, 512))
-        finish(slice(2, 4), slice(384, 512))
+                todo.remove((b, t))
+        for h, gs in [
+            (0, slice(0, 1)),
+            (0, slice(1, 2)),
+            (0, slice(2, 4)),
+            (1, slice(0, 2)),
+            (1, slice(2, 3)),
+            (1, slice(3, 4)),
+        ]:
+            finish(h, gs)

@@ -2,10 +2,11 @@ from contextlib import ExitStack
 
 import concourse.mybir as mybir
 
-G, D, M, N, L = 4, 128, 128, 512, 1024
+G, D, M, N = 4, 128, 128, 512
 TAPS = 5
-STEP = 128
-BLOCKS = N // STEP
+WIDTH = 128
+CHUNKS = N // WIDTH
+HALF = N // 2
 FLOPS = 2 * G * TAPS * D * M * N
 
 F32 = mybir.dt.float32
@@ -18,7 +19,20 @@ GELU = mybir.ActivationFunctionType.Gelu_apprx_tanh
 P = 128
 PACK = 4
 ROWS = D // PACK
-HALF = N // 2
+BANK = 512
+
+SHARED = 72
+STEPS = [
+    [(("w", 0), WIDTH)],
+    [(("x", 0), 0), (("x", 1), WIDTH)],
+    [(("x", 2), 0), (("w", 1), WIDTH)],
+    [(("x", 3), 0), (("w", 2), WIDTH)],
+    [(("x", 4), 0), (("w", 3), WIDTH)],
+    [(("w", 4), SHARED)],
+    [(("x", 5), SHARED)],
+    [(("x", 6), SHARED)],
+    [(("x", 7), WIDTH)],
+]
 
 
 def tile_rows_conv_res_kernel(tc, x, w0, w1, w2, w3, w4, r, out):
@@ -29,41 +43,31 @@ def tile_rows_conv_res_kernel(tc, x, w0, w1, w2, w3, w4, r, out):
         psum = ctx.enter_context(tc.psum_pool(name="psum", bufs=1))
         ctx.enter_context(tc.manual_schedule())
 
-        banks = [[psum.tile([M, 512], F32, name="bank%d_%d" % (g, s)) for s in range(2)] for g in range(G)]
+        banks = [[psum.tile([M, BANK], F32, name="bank%d_%d" % (g, h)) for h in range(2)] for g in range(G)]
 
         x_rows = x.rearrange("g (p j) l -> (g p) j l", j=PACK)
         w_rows = [w.rearrange("g (p j) m -> (g p) j m", j=PACK) for w in (w0, w1, w2, w3, w4)]
         r_rows = r.rearrange("g m n -> m g n")
-        out_rows = out.rearrange("g m n -> m g n")
 
         def load(name, rows):
             tile = sb.tile(list(rows.shape), F32, name=name)
             nc.sync.dma_start(out=tile[:], in_=rows)
             return tile
 
-        pairs = [
-            (("x", 0), ("x", 1)),
-            (("x", 2), ("w", 1)),
-            (("x", 3), ("w", 2)),
-            (("x", 4), ("w", 3)),
-            (("w", 4), ("x", 5)),
-            (("x", 6), ("x", 7)),
-        ]
-        raw = {}
-        raw["w", 0] = load("raw_w0", w_rows[0])[:]
-        first = load("raw_x01", x_rows[:, :, 0 : 2 * STEP])
-        raw["x", 0] = first[:, :, 0:STEP]
-        raw["x", 1] = first[:, :, STEP : 2 * STEP]
-        for pair in pairs[1:]:
-            for kind, i in pair:
-                rows = w_rows[i] if kind == "w" else x_rows[:, :, i * STEP : (i + 1) * STEP]
+        raw = {("w", 0): load("raw_w0", w_rows[0])[:]}
+        x_first = load("raw_x01", x_rows[:, :, 0 : 2 * WIDTH])
+        raw["x", 0] = x_first[:, :, 0:WIDTH]
+        raw["x", 1] = x_first[:, :, WIDTH : 2 * WIDTH]
+        for step in STEPS[2:]:
+            for (kind, i), vector_cols in step:
+                rows = w_rows[i] if kind == "w" else x_rows[:, :, i * WIDTH : (i + 1) * WIDTH]
                 raw[kind, i] = load("raw_%s%d" % (kind, i), rows)[:]
 
         res = sb.tile([M, G, N], F32, name="res")
         for h in range(2):
-            for gs in (slice(0, 2), slice(2, 4)):
-                cs = slice(h * HALF, (h + 1) * HALF)
-                nc.sync.dma_start(out=res[:, gs, cs], in_=r_rows[:, gs, cs])
+            for g in range(0, G, 2):
+                cols = slice(h * HALF, (h + 1) * HALF)
+                nc.sync.dma_start(out=res[:, g : g + 2, cols], in_=r_rows[:, g : g + 2, cols])
 
         zero = sb.tile([P, 8], F32, name="zero")
         bias = sb.tile([P, 8], F32, name="bias")
@@ -72,60 +76,52 @@ def tile_rows_conv_res_kernel(tc, x, w0, w1, w2, w3, w4, r, out):
 
         grouped, codes, scales = {}, {}, {}
 
-        def interleave(key, copy):
-            grouped[key] = sb.tile([P, STEP, PACK], BF16, name="grouped_%s%d" % key, align_bytes=64)
-            copy(out=grouped[key][:], in_=raw[key].rearrange("p j w -> p w j"))
+        def interleave(piece, vector_cols):
+            grouped[piece] = sb.tile([P, WIDTH, PACK], BF16, name="grouped_%s%d" % piece, align_bytes=64)
+            source = raw[piece].rearrange("p j c -> p c j")
+            if vector_cols < WIDTH:
+                nc.scalar.copy(out=grouped[piece][:, vector_cols:, :], in_=source[:, vector_cols:, :])
+            if vector_cols > 0:
+                nc.vector.tensor_copy(out=grouped[piece][:, :vector_cols, :], in_=source[:, :vector_cols, :])
 
-        def quantize(key):
-            codes[key] = sb.tile([P, STEP], U32, name="codes_%s%d" % key, align_bytes=64)
-            scales[key] = sb.tile([P, STEP], U8, name="scales_%s%d" % key, align_bytes=64)
+        def quantize(piece):
+            codes[piece] = sb.tile([P, WIDTH], U32, name="codes_%s%d" % piece, align_bytes=64)
+            scales[piece] = sb.tile([P, WIDTH], U8, name="scales_%s%d" % piece, align_bytes=64)
             nc.vector.quantize_mx(
-                out=codes[key][:].bitcast(FP8X4),
-                scales=scales[key][:],
-                in_=grouped[key][:].rearrange("p w j -> p (w j)"),
+                out=codes[piece][:].bitcast(FP8X4),
+                scales=scales[piece][:],
+                in_=grouped[piece][:].rearrange("p c j -> p (c j)"),
             )
 
         def multiply(b, t):
+            side = b % 2
             for g in range(G):
                 part = slice(g * ROWS, (g + 1) * ROWS)
                 nc.tensor.matmul_mx(
-                    out=banks[g][b // 2][:, (b % 2) * STEP : (b % 2 + 1) * STEP],
+                    out=banks[g][b // 2][:, side * WIDTH : (side + 1) * WIDTH],
                     lhsT=codes["w", t][part, :].bitcast(FP8X4),
                     lhsT_scale=scales["w", t][part, :],
                     rhs=codes["x", b + t][part, :].bitcast(FP8X4),
                     rhs_scale=scales["x", b + t][part, :],
-                    start=(t == 0 and b % 2 == 0),
-                    stop=(t == TAPS - 1 and b % 2 == 1),
+                    start=(t == 0 and side == 0),
+                    stop=(t == TAPS - 1 and side == 1),
                 )
 
-        act = sb.tile([M, G, N], F32, name="act")
-        y = sb.tile([M, G, N], F32, name="y")
-
-        def finish(h, gs):
-            cs = slice(h * HALF, (h + 1) * HALF)
-            for g in range(gs.start, gs.stop):
-                nc.scalar.activation(out=act[:, g, cs], in_=banks[g][h][:, 0:HALF], func=GELU, bias=bias[:, 0:1])
-            nc.vector.tensor_add(out=y[:, gs, cs], in0=act[:, gs, cs], in1=res[:, gs, cs])
-            nc.sync.dma_start(out=out_rows[:, gs, cs], in_=y[:, gs, cs])
-
-        interleave(("w", 0), nc.vector.tensor_copy)
-        quantize(("w", 0))
-        todo = [(b, t) for b in range(BLOCKS) for t in range(TAPS)]
-        for early, late in pairs:
-            interleave(early, nc.scalar.copy)
-            interleave(late, nc.vector.tensor_copy)
-            quantize(early)
-            quantize(late)
-            ready = [(b, t) for b, t in todo if ("w", t) in codes and ("x", b + t) in codes]
-            for b, t in ready:
+        todo = [(b, t) for b in range(CHUNKS) for t in range(TAPS)]
+        for step in STEPS:
+            for piece, vector_cols in step:
+                interleave(piece, vector_cols)
+            for piece, vector_cols in step:
+                quantize(piece)
+            for b, t in [(b, t) for b, t in todo if ("w", t) in codes and ("x", b + t) in codes]:
                 multiply(b, t)
                 todo.remove((b, t))
-        for h, gs in [
-            (0, slice(0, 1)),
-            (0, slice(1, 2)),
-            (0, slice(2, 4)),
-            (1, slice(0, 2)),
-            (1, slice(2, 3)),
-            (1, slice(3, 4)),
-        ]:
-            finish(h, gs)
+
+        for h in range(2):
+            cols = slice(h * HALF, (h + 1) * HALF)
+            for g in range(G):
+                act = sb.tile([M, HALF], F32, name="act%d_%d" % (g, h))
+                y = sb.tile([M, HALF], F32, name="y%d_%d" % (g, h))
+                nc.scalar.activation(out=act[:], in_=banks[g][h][:, 0:HALF], func=GELU, bias=bias[:, 0:1])
+                nc.vector.tensor_add(out=y[:], in0=act[:], in1=res[:, g, cols])
+                nc.sync.dma_start(out=out[g, :, cols], in_=y[:])

@@ -21,17 +21,16 @@ PACK = 4
 ROWS = D // PACK
 BANK = 512
 
+LOADS = [("w", 0, 1), ("x", 0, 4), ("w", 1, 1), ("w", 2, 1), ("x", 4, 2), ("w", 3, 1), ("w", 4, 1), ("x", 6, 2)]
 SHARED = 72
+EARLY = 80
 STEPS = [
-    [(("w", 0), WIDTH)],
-    [(("x", 0), 0), (("x", 1), WIDTH)],
-    [(("x", 2), 0), (("w", 1), WIDTH)],
-    [(("x", 3), 0), (("w", 2), WIDTH)],
-    [(("x", 4), 0), (("w", 3), WIDTH)],
-    [(("w", 4), SHARED)],
-    [(("x", 5), SHARED)],
-    [(("x", 6), SHARED)],
-    [(("x", 7), WIDTH)],
+    [(("w", 0), SHARED)],
+    [(("x", 0), WIDTH), (("x", 1), 0), (("x", 2), WIDTH), (("x", 3), 0)],
+    [(("w", 1), WIDTH), (("w", 2), 0)],
+    [(("x", 4), WIDTH), (("x", 5), 0)],
+    [(("w", 3), 0), (("w", 4), WIDTH)],
+    [(("x", 6), EARLY), (("x", 7), WIDTH)],
 ]
 
 
@@ -54,14 +53,12 @@ def tile_rows_conv_res_kernel(tc, x, w0, w1, w2, w3, w4, r, out):
             nc.sync.dma_start(out=tile[:], in_=rows)
             return tile
 
-        raw = {("w", 0): load("raw_w0", w_rows[0])[:]}
-        x_first = load("raw_x01", x_rows[:, :, 0 : 2 * WIDTH])
-        raw["x", 0] = x_first[:, :, 0:WIDTH]
-        raw["x", 1] = x_first[:, :, WIDTH : 2 * WIDTH]
-        for step in STEPS[2:]:
-            for (kind, i), vector_cols in step:
-                rows = w_rows[i] if kind == "w" else x_rows[:, :, i * WIDTH : (i + 1) * WIDTH]
-                raw[kind, i] = load("raw_%s%d" % (kind, i), rows)[:]
+        raw = {}
+        for kind, first, count in LOADS:
+            rows = w_rows[first] if kind == "w" else x_rows[:, :, first * WIDTH : (first + count) * WIDTH]
+            tile = load("raw_%s%d" % (kind, first), rows)
+            for i in range(count):
+                raw[kind, first + i] = tile[:, :, i * WIDTH : (i + 1) * WIDTH]
 
         res = sb.tile([M, G, N], F32, name="res")
         for h in range(2):
@@ -113,9 +110,9 @@ def tile_rows_conv_res_kernel(tc, x, w0, w1, w2, w3, w4, r, out):
                 interleave(piece, vector_cols)
             for piece, vector_cols in step:
                 quantize(piece)
-            for b, t in [(b, t) for b, t in todo if ("w", t) in codes and ("x", b + t) in codes]:
-                multiply(b, t)
-                todo.remove((b, t))
+                for b, t in [(b, t) for b, t in todo if ("w", t) in codes and ("x", b + t) in codes]:
+                    multiply(b, t)
+                    todo.remove((b, t))
 
         for h in range(2):
             cols = slice(h * HALF, (h + 1) * HALF)

@@ -22,14 +22,15 @@ ROWS = D // PACK
 BANK = 512
 
 LOADS = [("w", 0, 1), ("x", 0, 4), ("w", 1, 1), ("w", 2, 1), ("x", 4, 2), ("w", 3, 1), ("w", 4, 1), ("x", 6, 2)]
+RUN = 4
 SHARED = 72
-EARLY = 80
+EARLY = 56
 STEPS = [
     [(("w", 0), SHARED)],
     [(("x", 0), WIDTH), (("x", 1), 0), (("x", 2), WIDTH), (("x", 3), 0)],
     [(("w", 1), WIDTH), (("w", 2), 0)],
     [(("x", 4), WIDTH), (("x", 5), 0)],
-    [(("w", 3), 0), (("w", 4), WIDTH)],
+    [(("w", 3), 0), (("w", 4), SHARED)],
     [(("x", 6), EARLY), (("x", 7), WIDTH)],
 ]
 
@@ -75,11 +76,13 @@ def tile_rows_conv_res_kernel(tc, x, w0, w1, w2, w3, w4, r, out):
 
         def interleave(piece, vector_cols):
             grouped[piece] = sb.tile([P, WIDTH, PACK], BF16, name="grouped_%s%d" % piece, align_bytes=64)
-            source = raw[piece].rearrange("p j c -> p c j")
+            source = raw[piece].rearrange("p j (c i) -> p c j i", i=RUN)
+            target = grouped[piece][:].rearrange("p (c i) j -> p c j i", i=RUN)
+            split = vector_cols // RUN
             if vector_cols < WIDTH:
-                nc.scalar.copy(out=grouped[piece][:, vector_cols:, :], in_=source[:, vector_cols:, :])
+                nc.scalar.copy(out=target[:, split:, :, :], in_=source[:, split:, :, :])
             if vector_cols > 0:
-                nc.vector.tensor_copy(out=grouped[piece][:, :vector_cols, :], in_=source[:, :vector_cols, :])
+                nc.vector.tensor_copy(out=target[:, :split, :, :], in_=source[:, :split, :, :])
 
         def quantize(piece):
             codes[piece] = sb.tile([P, WIDTH], U32, name="codes_%s%d" % piece, align_bytes=64)
@@ -104,15 +107,15 @@ def tile_rows_conv_res_kernel(tc, x, w0, w1, w2, w3, w4, r, out):
                     stop=(t == TAPS - 1 and side == 1),
                 )
 
-        todo = [(b, t) for b in range(CHUNKS) for t in range(TAPS)]
+        todo = [(b, t) for h in range(2) for t in range(TAPS) for b in (2 * h, 2 * h + 1)]
         for step in STEPS:
             for piece, vector_cols in step:
                 interleave(piece, vector_cols)
             for piece, vector_cols in step:
                 quantize(piece)
-                for b, t in [(b, t) for b, t in todo if ("w", t) in codes and ("x", b + t) in codes]:
-                    multiply(b, t)
-                    todo.remove((b, t))
+            for b, t in [(b, t) for b, t in todo if ("w", t) in codes and ("x", b + t) in codes]:
+                multiply(b, t)
+                todo.remove((b, t))
 
         for h in range(2):
             cols = slice(h * HALF, (h + 1) * HALF)

@@ -21,17 +21,18 @@ PACK = 4
 ROWS = D // PACK
 BANK = 512
 
-LOADS = [("w", 0, 1), ("x", 0, 4), ("w", 1, 1), ("w", 2, 1), ("x", 4, 2), ("w", 3, 1), ("w", 4, 1), ("x", 6, 2)]
+LOADS = [("x", 0, 6), ("w", 0, 1), ("w", 1, 1), ("w", 2, 1), ("w", 3, 1), ("w", 4, 1), ("x", 6, 2)]
 RUN = 4
 SHARED = 72
 EARLY = 56
 STEPS = [
-    [(("w", 0), SHARED)],
-    [(("x", 0), WIDTH), (("x", 1), 0), (("x", 2), WIDTH), (("x", 3), 0)],
-    [(("w", 1), WIDTH), (("w", 2), 0)],
-    [(("x", 4), WIDTH), (("x", 5), 0)],
-    [(("w", 3), 0), (("w", 4), SHARED)],
-    [(("x", 6), EARLY), (("x", 7), WIDTH)],
+    ([(("x", 0), WIDTH), (("x", 1), 0), (("x", 2), WIDTH)], [("x", 0)]),
+    ([(("w", 0), WIDTH), (("x", 3), 0)], [("x", 1), ("x", 2)]),
+    ([(("w", 1), WIDTH), (("x", 4), 0)], [("w", 0), ("x", 3)]),
+    ([(("w", 2), WIDTH), (("x", 5), 0)], [("w", 1), ("x", 4)]),
+    ([(("w", 3), 0)], [("w", 2), ("x", 5)]),
+    ([(("w", 4), SHARED)], [("w", 3), ("w", 4)]),
+    ([(("x", 6), EARLY), (("x", 7), WIDTH)], [("x", 6), ("x", 7)]),
 ]
 
 
@@ -108,10 +109,10 @@ def tile_rows_conv_res_kernel(tc, x, w0, w1, w2, w3, w4, r, out):
                 )
 
         todo = [(b, t) for h in range(2) for t in range(TAPS) for b in (2 * h, 2 * h + 1)]
-        for step in STEPS:
-            for piece, vector_cols in step:
+        for copies, ready in STEPS:
+            for piece, vector_cols in copies:
                 interleave(piece, vector_cols)
-            for piece, vector_cols in step:
+            for piece in ready:
                 quantize(piece)
             for b, t in [(b, t) for b, t in todo if ("w", t) in codes and ("x", b + t) in codes]:
                 multiply(b, t)

@@ -15,6 +15,7 @@ U32 = mybir.dt.uint32
 U8 = mybir.dt.uint8
 FP8X4 = mybir.dt.float8_e4m3fn_x4
 GELU = mybir.ActivationFunctionType.Gelu_apprx_tanh
+IDENTITY = mybir.ActivationFunctionType.Identity
 
 P = 128
 PACK = 4
@@ -23,6 +24,7 @@ BANK = 512
 
 LOADS = [("x", 0, 6), ("w", 0, 1), ("w", 1, 1), ("w", 2, 1), ("w", 3, 1), ("w", 4, 1), ("x", 6, 2)]
 RUN = 4
+FIRST_ON_SCALAR = ("x", 1)
 SHARED = 72
 EARLY = 56
 STEPS = [
@@ -80,7 +82,9 @@ def tile_rows_conv_res_kernel(tc, x, w0, w1, w2, w3, w4, r, out):
             source = raw[piece].rearrange("p j (c i) -> p c j i", i=RUN)
             target = grouped[piece][:].rearrange("p (c i) j -> p c j i", i=RUN)
             split = vector_cols // RUN
-            if vector_cols < WIDTH:
+            if piece == FIRST_ON_SCALAR:
+                nc.scalar.activation(out=target, in_=source, func=IDENTITY, bias=bias[:, 0:1])
+            elif vector_cols < WIDTH:
                 nc.scalar.copy(out=target[:, split:, :, :], in_=source[:, split:, :, :])
             if vector_cols > 0:
                 nc.vector.tensor_copy(out=target[:, :split, :, :], in_=source[:, :split, :, :])
@@ -118,11 +122,17 @@ def tile_rows_conv_res_kernel(tc, x, w0, w1, w2, w3, w4, r, out):
                 multiply(b, t)
                 todo.remove((b, t))
 
+        late = []
         for h in range(2):
             cols = slice(h * HALF, (h + 1) * HALF)
             for g in range(G):
                 act = sb.tile([M, HALF], F32, name="act%d_%d" % (g, h))
                 y = sb.tile([M, HALF], F32, name="y%d_%d" % (g, h))
-                nc.scalar.activation(out=act[:], in_=banks[g][h][:, 0:HALF], func=GELU, bias=bias[:, 0:1])
+                nc.scalar.activation(out=act[:], in_=banks[g][h][:, 0:HALF], func=GELU)
                 nc.vector.tensor_add(out=y[:], in0=act[:], in1=res[:, g, cols])
-                nc.sync.dma_start(out=out[g, :, cols], in_=y[:])
+                if h == 1 and g % 2 == 1:
+                    late.append((out[g, :, cols], y))
+                else:
+                    nc.sync.dma_start(out=out[g, :, cols], in_=y[:])
+        for rows, y in late:
+            nc.scalar.dma_start(out=rows, in_=y[:])

@@ -23,7 +23,7 @@ ROWS = D // PACK
 BANK = 512
 
 LOADS = [("x", 0, 6), ("w", 0, 1), ("w", 1, 1), ("w", 2, 1), ("w", 3, 1), ("w", 4, 1), ("x", 6, 2)]
-RUN = 4
+RUN = 2
 FIRST_ON_SCALAR = ("x", 1)
 SHARED = 72
 EARLY = 56
@@ -122,7 +122,6 @@ def tile_rows_conv_res_kernel(tc, x, w0, w1, w2, w3, w4, r, out):
                 multiply(b, t)
                 todo.remove((b, t))
 
-        late = []
         for h in range(2):
             cols = slice(h * HALF, (h + 1) * HALF)
             for g in range(G):
@@ -130,9 +129,4 @@ def tile_rows_conv_res_kernel(tc, x, w0, w1, w2, w3, w4, r, out):
                 y = sb.tile([M, HALF], F32, name="y%d_%d" % (g, h))
                 nc.scalar.activation(out=act[:], in_=banks[g][h][:, 0:HALF], func=GELU)
                 nc.vector.tensor_add(out=y[:], in0=act[:], in1=res[:, g, cols])
-                if h == 1 and g % 2 == 1:
-                    late.append((out[g, :, cols], y))
-                else:
-                    nc.sync.dma_start(out=out[g, :, cols], in_=y[:])
-        for rows, y in late:
-            nc.scalar.dma_start(out=rows, in_=y[:])
+                nc.sync.dma_start(out=out[g, :, cols], in_=y[:])

@@ -22,19 +22,28 @@ PACK = 4
 ROWS = D // PACK
 BANK = 512
 
-LOADS = [("x", 0, 6), ("w", 0, 1), ("w", 1, 1), ("w", 2, 1), ("w", 3, 1), ("w", 4, 1), ("x", 6, 2)]
+CUT = 768
 RUN = 2
-FIRST_ON_SCALAR = ("x", 1)
+LOW, HIGH, ALL = (0, 2), (2, 4), (0, 4)
+FIRST_ON_SCALAR = (("x", 1), LOW)
 SHARED = 72
 EARLY = 56
+
+V, S = "vector", "scalar"
 STEPS = [
-    ([(("x", 0), WIDTH), (("x", 1), 0), (("x", 2), WIDTH)], [("x", 0)]),
-    ([(("w", 0), WIDTH), (("x", 3), 0)], [("x", 1), ("x", 2)]),
-    ([(("w", 1), WIDTH), (("x", 4), 0)], [("w", 0), ("x", 3)]),
-    ([(("w", 2), WIDTH), (("x", 5), 0)], [("w", 1), ("x", 4)]),
-    ([(("w", 3), 0)], [("w", 2), ("x", 5)]),
-    ([(("w", 4), SHARED)], [("w", 3), ("w", 4)]),
-    ([(("x", 6), EARLY), (("x", 7), WIDTH)], [("x", 6), ("x", 7)]),
+    ([(("w", 0), ALL, V, 0, WIDTH)] + [(("x", c), LOW, (V, S)[c % 2], 0, WIDTH) for c in range(6)], [("w", 0)]),
+    (
+        [(("x", 0), HIGH, V, 0, WIDTH), (("x", 1), HIGH, S, 0, WIDTH), (("x", 2), HIGH, V, 0, WIDTH)],
+        [("x", 0)],
+    ),
+    ([(("w", 1), ALL, V, 0, WIDTH), (("x", 3), HIGH, S, 0, WIDTH)], [("x", 1), ("x", 2)]),
+    ([(("w", 2), ALL, V, 0, WIDTH), (("x", 4), HIGH, S, 0, WIDTH)], [("w", 1), ("x", 3)]),
+    ([(("x", 5), HIGH, S, 0, WIDTH), (("w", 3), ALL, S, 0, WIDTH)], [("w", 2), ("x", 4), ("x", 5)]),
+    ([(("w", 4), ALL, S, SHARED, WIDTH), (("w", 4), ALL, V, 0, SHARED)], [("w", 3), ("w", 4)]),
+    (
+        [(("x", 6), ALL, S, EARLY, WIDTH), (("x", 6), ALL, V, 0, EARLY), (("x", 7), ALL, V, 0, WIDTH)],
+        [("x", 6), ("x", 7)],
+    ),
 ]
 
 
@@ -57,12 +66,19 @@ def tile_rows_conv_res_kernel(tc, x, w0, w1, w2, w3, w4, r, out):
             nc.sync.dma_start(out=tile[:], in_=rows)
             return tile
 
-        raw = {}
-        for kind, first, count in LOADS:
-            rows = w_rows[first] if kind == "w" else x_rows[:, :, first * WIDTH : (first + count) * WIDTH]
-            tile = load("raw_%s%d" % (kind, first), rows)
-            for i in range(count):
-                raw[kind, first + i] = tile[:, :, i * WIDTH : (i + 1) * WIDTH]
+        w_raw = [load("w_raw0", w_rows[0])]
+        x_first = {rows: load("x_first%d" % rows[0], x_rows[:, rows[0] : rows[1], 0:CUT]) for rows in (LOW, HIGH)}
+        w_raw += [load("w_raw%d" % t, w_rows[t]) for t in range(1, TAPS)]
+        x_last = load("x_last", x_rows[:, :, CUT:])
+
+        def raw(piece, rows, first, end):
+            kind, index = piece
+            if kind == "w":
+                return w_raw[index][:, :, first:end]
+            at = index * WIDTH
+            if at + end <= CUT:
+                return x_first[rows][:, :, at + first : at + end]
+            return x_last[:, :, at + first - CUT : at + end - CUT]
 
         res = sb.tile([M, G, N], F32, name="res")
         for h in range(2):
@@ -77,17 +93,17 @@ def tile_rows_conv_res_kernel(tc, x, w0, w1, w2, w3, w4, r, out):
 
         grouped, codes, scales = {}, {}, {}
 
-        def interleave(piece, vector_cols):
-            grouped[piece] = sb.tile([P, WIDTH, PACK], BF16, name="grouped_%s%d" % piece, align_bytes=64)
-            source = raw[piece].rearrange("p j (c i) -> p c j i", i=RUN)
-            target = grouped[piece][:].rearrange("p (c i) j -> p c j i", i=RUN)
-            split = vector_cols // RUN
-            if piece == FIRST_ON_SCALAR:
+        def interleave(piece, rows, engine, first, end):
+            if piece not in grouped:
+                grouped[piece] = sb.tile([P, WIDTH, PACK], BF16, name="grouped_%s%d" % piece, align_bytes=64)
+            source = raw(piece, rows, first, end).rearrange("p j (c i) -> p c j i", i=RUN)
+            target = grouped[piece][:, first:end, rows[0] : rows[1]].rearrange("p (c i) j -> p c j i", i=RUN)
+            if (piece, rows) == FIRST_ON_SCALAR:
                 nc.scalar.activation(out=target, in_=source, func=IDENTITY, bias=bias[:, 0:1])
-            elif vector_cols < WIDTH:
-                nc.scalar.copy(out=target[:, split:, :, :], in_=source[:, split:, :, :])
-            if vector_cols > 0:
-                nc.vector.tensor_copy(out=target[:, :split, :, :], in_=source[:, :split, :, :])
+            elif engine == S:
+                nc.scalar.copy(out=target, in_=source)
+            else:
+                nc.vector.tensor_copy(out=target, in_=source)
 
         def quantize(piece):
             codes[piece] = sb.tile([P, WIDTH], U32, name="codes_%s%d" % piece, align_bytes=64)
@@ -114,8 +130,8 @@ def tile_rows_conv_res_kernel(tc, x, w0, w1, w2, w3, w4, r, out):
 
         todo = [(b, t) for h in range(2) for t in range(TAPS) for b in (2 * h, 2 * h + 1)]
         for copies, ready in STEPS:
-            for piece, vector_cols in copies:
-                interleave(piece, vector_cols)
+            for copy in copies:
+                interleave(*copy)
             for piece in ready:
                 quantize(piece)
             for b, t in [(b, t) for b, t in todo if ("w", t) in codes and ("x", b + t) in codes]:

@@ -2,7 +2,7 @@ from contextlib import ExitStack
 
 import concourse.mybir as mybir
 
-G, D, M, N = 4, 128, 128, 512
+G, D, M, N, L = 4, 128, 128, 512, 1024
 TAPS = 5
 WIDTH = 128
 CHUNKS = N // WIDTH
@@ -22,28 +22,30 @@ PACK = 4
 ROWS = D // PACK
 BANK = 512
 
-CUT = 768
 RUN = 2
-LOW, HIGH, ALL = (0, 2), (2, 4), (0, 4)
-FIRST_ON_SCALAR = (("x", 1), LOW)
-SHARED = 72
-EARLY = 56
-
+CUT = 768
+LOW, HIGH, ALL = slice(0, 2), slice(2, 4), slice(0, 4)
+ROW0, ROW2, ODD = slice(0, 1), slice(2, 3), slice(1, 4, 2)
 V, S = "vector", "scalar"
+SHARED = 72
+EARLY = 64
+FIRST_ON_SCALAR = (("x", 1), LOW)
+
+def tail(rows):
+    return [(("x", 6), rows, S, EARLY, WIDTH), (("x", 6), rows, V, 0, EARLY), (("x", 7), rows, V, 0, WIDTH)]
+
+
 STEPS = [
-    ([(("w", 0), ALL, V, 0, WIDTH)] + [(("x", c), LOW, (V, S)[c % 2], 0, WIDTH) for c in range(6)], [("w", 0)]),
+    ([(("x", c), LOW, (V, S)[c % 2], 0, WIDTH) for c in range(6)] + tail(ROW0), []),
+    ([(("x", c), HIGH, (V, S)[c % 2], 0, WIDTH) for c in range(6)], []),
     (
-        [(("x", 0), HIGH, V, 0, WIDTH), (("x", 1), HIGH, S, 0, WIDTH), (("x", 2), HIGH, V, 0, WIDTH)],
-        [("x", 0)],
+        [(("w", 0), ALL, V, 0, WIDTH), (("w", 1), ALL, S, 0, WIDTH)],
+        [("x", 0), ("x", 1), ("x", 2), ("w", 0), ("x", 3), ("x", 4)],
     ),
-    ([(("w", 1), ALL, V, 0, WIDTH), (("x", 3), HIGH, S, 0, WIDTH)], [("x", 1), ("x", 2)]),
-    ([(("w", 2), ALL, V, 0, WIDTH), (("x", 4), HIGH, S, 0, WIDTH)], [("w", 1), ("x", 3)]),
-    ([(("x", 5), HIGH, S, 0, WIDTH), (("w", 3), ALL, S, 0, WIDTH)], [("w", 2), ("x", 4), ("x", 5)]),
+    ([(("w", 2), ALL, V, 0, WIDTH)], [("w", 1), ("x", 5), ("w", 2)]),
+    (tail(ROW2) + [(("w", 3), ALL, S, 0, WIDTH)], []),
     ([(("w", 4), ALL, S, SHARED, WIDTH), (("w", 4), ALL, V, 0, SHARED)], [("w", 3), ("w", 4)]),
-    (
-        [(("x", 6), ALL, S, EARLY, WIDTH), (("x", 6), ALL, V, 0, EARLY), (("x", 7), ALL, V, 0, WIDTH)],
-        [("x", 6), ("x", 7)],
-    ),
+    (tail(ODD), [("x", 6), ("x", 7)]),
 ]
 
 
@@ -57,34 +59,38 @@ def tile_rows_conv_res_kernel(tc, x, w0, w1, w2, w3, w4, r, out):
 
         banks = [[psum.tile([M, BANK], F32, name="bank%d_%d" % (g, h)) for h in range(2)] for g in range(G)]
 
-        x_rows = x.rearrange("g (p j) l -> (g p) j l", j=PACK)
-        w_rows = [w.rearrange("g (p j) m -> (g p) j m", j=PACK) for w in (w0, w1, w2, w3, w4)]
-        r_rows = r.rearrange("g m n -> m g n")
-
         def load(name, rows):
             tile = sb.tile(list(rows.shape), F32, name=name)
             nc.sync.dma_start(out=tile[:], in_=rows)
             return tile
 
-        w_raw = [load("w_raw0", w_rows[0])]
-        x_first = {rows: load("x_first%d" % rows[0], x_rows[:, rows[0] : rows[1], 0:CUT]) for rows in (LOW, HIGH)}
-        w_raw += [load("w_raw%d" % t, w_rows[t]) for t in range(1, TAPS)]
-        x_last = load("x_last", x_rows[:, :, CUT:])
+        x_pairs = x.rearrange("g (p u e) l -> (g p) u (e l)", u=2, e=2)
+        x_run = []
+        for u in range(2):
+            tile = sb.tile([P, 2 * L], F32, name="x_run%d" % u)
+            nc.sync.dma_start(out=tile[:, 0 : L + CUT], in_=x_pairs[:, u, 0 : L + CUT])
+            x_run.append(tile[:].rearrange("p (e l) -> p e l", e=2))
+        w_raw = [
+            load("w_raw%d" % t, w.rearrange("g (p j) m -> (g p) j m", j=PACK)) for t, w in enumerate((w0, w1, w2, w3, w4))
+        ]
+        x_ends = load("x_ends", x_pairs[:, :, L + CUT :])
 
         def raw(piece, rows, first, end):
             kind, index = piece
             if kind == "w":
                 return w_raw[index][:, :, first:end]
             at = index * WIDTH
-            if at + end <= CUT:
-                return x_first[rows][:, :, at + first : at + end]
-            return x_last[:, :, at + first - CUT : at + end - CUT]
+            if rows == ODD:
+                return x_ends[:, :, at + first - CUT : at + end - CUT]
+            return x_run[rows.start // 2][:, 0 : rows.stop - rows.start, at + first : at + end]
 
-        res = sb.tile([M, G, N], F32, name="res")
+        r_rows = r.rearrange("g m n -> m g n")
+        res = {}
         for h in range(2):
-            for g in range(0, G, 2):
-                cols = slice(h * HALF, (h + 1) * HALF)
-                nc.sync.dma_start(out=res[:, g : g + 2, cols], in_=r_rows[:, g : g + 2, cols])
+            for first in range(0, G, 2):
+                tile = load("res%d_%d" % (first, h), r_rows[:, first : first + 2, h * HALF : (h + 1) * HALF])
+                for g in (first, first + 1):
+                    res[g, h] = tile[:, g - first, :]
 
         zero = sb.tile([P, 8], F32, name="zero")
         bias = sb.tile([P, 8], F32, name="bias")
@@ -97,7 +103,7 @@ def tile_rows_conv_res_kernel(tc, x, w0, w1, w2, w3, w4, r, out):
             if piece not in grouped:
                 grouped[piece] = sb.tile([P, WIDTH, PACK], BF16, name="grouped_%s%d" % piece, align_bytes=64)
             source = raw(piece, rows, first, end).rearrange("p j (c i) -> p c j i", i=RUN)
-            target = grouped[piece][:, first:end, rows[0] : rows[1]].rearrange("p (c i) j -> p c j i", i=RUN)
+            target = grouped[piece][:, first:end, rows].rearrange("p (c i) j -> p c j i", i=RUN)
             if (piece, rows) == FIRST_ON_SCALAR:
                 nc.scalar.activation(out=target, in_=source, func=IDENTITY, bias=bias[:, 0:1])
             elif engine == S:
@@ -144,5 +150,5 @@ def tile_rows_conv_res_kernel(tc, x, w0, w1, w2, w3, w4, r, out):
                 act = sb.tile([M, HALF], F32, name="act%d_%d" % (g, h))
                 y = sb.tile([M, HALF], F32, name="y%d_%d" % (g, h))
                 nc.scalar.activation(out=act[:], in_=banks[g][h][:, 0:HALF], func=GELU)
-                nc.vector.tensor_add(out=y[:], in0=act[:], in1=res[:, g, cols])
+                nc.vector.tensor_add(out=y[:], in0=act[:], in1=res[g, h])
                 nc.sync.dma_start(out=out[g, :, cols], in_=y[:])

@@ -24,29 +24,29 @@ BANK = 512
 
 RUN = 2
 CUT = 768
-LOW, HIGH, ALL = slice(0, 2), slice(2, 4), slice(0, 4)
-ROW0, ROW2, ODD = slice(0, 1), slice(2, 3), slice(1, 4, 2)
+ALL, EVEN, ODD = slice(0, 4), slice(0, 4, 2), slice(1, 4, 2)
 V, S = "vector", "scalar"
 SHARED = 72
-EARLY = 64
-FIRST_ON_SCALAR = (("x", 1), LOW)
+EARLY = 32
+HELD_FROM = 2
+FIRST_ON_SCALAR = (("x", 1), ALL)
 
 def tail(rows):
     return [(("x", 6), rows, S, EARLY, WIDTH), (("x", 6), rows, V, 0, EARLY), (("x", 7), rows, V, 0, WIDTH)]
 
 
 STEPS = [
-    ([(("x", c), LOW, (V, S)[c % 2], 0, WIDTH) for c in range(6)] + tail(ROW0), []),
-    ([(("x", c), HIGH, (V, S)[c % 2], 0, WIDTH) for c in range(6)], []),
-    (
-        [(("w", 0), ALL, V, 0, WIDTH), (("w", 1), ALL, S, 0, WIDTH)],
-        [("x", 0), ("x", 1), ("x", 2), ("w", 0), ("x", 3), ("x", 4)],
-    ),
-    ([(("w", 2), ALL, V, 0, WIDTH)], [("w", 1), ("x", 5), ("w", 2)]),
-    (tail(ROW2) + [(("w", 3), ALL, S, 0, WIDTH)], []),
+    ([(("x", 0), ALL, V, 0, WIDTH), (("x", 1), ALL, S, 0, WIDTH), (("x", 2), ALL, V, 0, WIDTH)], [("x", 0)]),
+    ([(("w", 0), ALL, V, 0, WIDTH), (("x", 3), ALL, S, 0, WIDTH)], [("x", 1), ("x", 2)]),
+    ([(("w", 1), ALL, V, 0, WIDTH), (("x", 4), ALL, S, 0, WIDTH)], [("w", 0), ("x", 3)]),
+    ([(("w", 2), ALL, V, 0, WIDTH), (("x", 5), ALL, S, 0, WIDTH)], [("w", 1), ("x", 4)]),
+    ([(("w", 3), ALL, S, 0, WIDTH)], [("w", 2), ("x", 5)]),
     ([(("w", 4), ALL, S, SHARED, WIDTH), (("w", 4), ALL, V, 0, SHARED)], [("w", 3), ("w", 4)]),
-    (tail(ODD), [("x", 6), ("x", 7)]),
+    (tail(EVEN) + tail(ODD), [("x", 6), ("x", 7)]),
 ]
+
+RESIDUAL_BLOCKS = [(0, 2, 0, 1), (2, 3, 0, 2), (3, 4, 0, 2), (0, 2, 1, 2)]
+OUT_BLOCKS = [(0, 1, 0, 1), (1, 2, 0, 1), (2, 3, 0, 2), (3, 4, 0, 2), (0, 2, 1, 2)]
 
 
 def tile_rows_conv_res_kernel(tc, x, w0, w1, w2, w3, w4, r, out):
@@ -65,11 +65,9 @@ def tile_rows_conv_res_kernel(tc, x, w0, w1, w2, w3, w4, r, out):
             return tile
 
         x_pairs = x.rearrange("g (p u e) l -> (g p) u (e l)", u=2, e=2)
-        x_run = []
-        for u in range(2):
-            tile = sb.tile([P, 2 * L], F32, name="x_run%d" % u)
-            nc.sync.dma_start(out=tile[:, 0 : L + CUT], in_=x_pairs[:, u, 0 : L + CUT])
-            x_run.append(tile[:].rearrange("p (e l) -> p e l", e=2))
+        x_runs = sb.tile([P, 2, 2 * L], F32, name="x_runs")
+        nc.sync.dma_start(out=x_runs[:, :, 0 : L + CUT], in_=x_pairs[:, :, 0 : L + CUT])
+        x_early = x_runs[:].rearrange("p u (e l) -> p (u e) l", e=2)
         w_raw = [
             load("w_raw%d" % t, w.rearrange("g (p j) m -> (g p) j m", j=PACK)) for t, w in enumerate((w0, w1, w2, w3, w4))
         ]
@@ -82,15 +80,15 @@ def tile_rows_conv_res_kernel(tc, x, w0, w1, w2, w3, w4, r, out):
             at = index * WIDTH
             if rows == ODD:
                 return x_ends[:, :, at + first - CUT : at + end - CUT]
-            return x_run[rows.start // 2][:, 0 : rows.stop - rows.start, at + first : at + end]
+            return x_early[:, rows, at + first : at + end]
 
         r_rows = r.rearrange("g m n -> m g n")
         res = {}
-        for h in range(2):
-            for first in range(0, G, 2):
-                tile = load("res%d_%d" % (first, h), r_rows[:, first : first + 2, h * HALF : (h + 1) * HALF])
-                for g in (first, first + 1):
-                    res[g, h] = tile[:, g - first, :]
+        for g0, g1, h0, h1 in RESIDUAL_BLOCKS:
+            tile = load("res%d_%d" % (g0, h0), r_rows[:, g0:g1, h0 * HALF : h1 * HALF])
+            for g in range(g0, g1):
+                for h in range(h0, h1):
+                    res[g, h] = tile[:, g - g0, (h - h0) * HALF : (h - h0 + 1) * HALF]
 
         zero = sb.tile([P, 8], F32, name="zero")
         bias = sb.tile([P, 8], F32, name="bias")
@@ -134,21 +132,27 @@ def tile_rows_conv_res_kernel(tc, x, w0, w1, w2, w3, w4, r, out):
                     stop=(t == TAPS - 1 and side == 1),
                 )
 
+        def ready_for(b, t):
+            held = b >= 2 and t >= HELD_FROM and ("w", TAPS - 1) not in codes
+            return ("w", t) in codes and ("x", b + t) in codes and not held
+
         todo = [(b, t) for h in range(2) for t in range(TAPS) for b in (2 * h, 2 * h + 1)]
         for copies, ready in STEPS:
             for copy in copies:
                 interleave(*copy)
             for piece in ready:
                 quantize(piece)
-            for b, t in [(b, t) for b, t in todo if ("w", t) in codes and ("x", b + t) in codes]:
+            for b, t in [(b, t) for b, t in todo if ready_for(b, t)]:
                 multiply(b, t)
                 todo.remove((b, t))
 
-        for h in range(2):
-            cols = slice(h * HALF, (h + 1) * HALF)
-            for g in range(G):
-                act = sb.tile([M, HALF], F32, name="act%d_%d" % (g, h))
-                y = sb.tile([M, HALF], F32, name="y%d_%d" % (g, h))
-                nc.scalar.activation(out=act[:], in_=banks[g][h][:, 0:HALF], func=GELU)
-                nc.vector.tensor_add(out=y[:], in0=act[:], in1=res[g, h])
-                nc.sync.dma_start(out=out[g, :, cols], in_=y[:])
+        out_rows = out.rearrange("g m n -> m g n")
+        for g0, g1, h0, h1 in OUT_BLOCKS:
+            y = sb.tile([M, g1 - g0, (h1 - h0) * HALF], F32, name="y%d_%d" % (g0, h0))
+            for g in range(g0, g1):
+                for h in range(h0, h1):
+                    act = sb.tile([M, HALF], F32, name="act%d_%d" % (g, h))
+                    nc.scalar.activation(out=act[:], in_=banks[g][h][:, 0:HALF], func=GELU)
+                    cols = slice((h - h0) * HALF, (h - h0 + 1) * HALF)
+                    nc.vector.tensor_add(out=y[:, g - g0, cols], in0=act[:], in1=res[g, h])
+            nc.sync.dma_start(out=out_rows[:, g0:g1, h0 * HALF : h1 * HALF], in_=y[:])

@@ -21,6 +21,7 @@ P = 128
 PACK = 4
 ROWS = D // PACK
 BANK = 512
+ALIGN = 256
 
 RUN = 2
 CUT = 768
@@ -60,12 +61,12 @@ def tile_rows_conv_res_kernel(tc, x, w0, w1, w2, w3, w4, r, out):
         banks = [[psum.tile([M, BANK], F32, name="bank%d_%d" % (g, h)) for h in range(2)] for g in range(G)]
 
         def load(name, rows):
-            tile = sb.tile(list(rows.shape), F32, name=name)
+            tile = sb.tile(list(rows.shape), F32, name=name, align_bytes=ALIGN)
             nc.sync.dma_start(out=tile[:], in_=rows)
             return tile
 
         x_pairs = x.rearrange("g (p u e) l -> (g p) u (e l)", u=2, e=2)
-        x_runs = sb.tile([P, 2, 2 * L], F32, name="x_runs")
+        x_runs = sb.tile([P, 2, 2 * L], F32, name="x_runs", align_bytes=ALIGN)
         nc.sync.dma_start(out=x_runs[:, :, 0 : L + CUT], in_=x_pairs[:, :, 0 : L + CUT])
         x_early = x_runs[:].rearrange("p u (e l) -> p (u e) l", e=2)
         w_raw = [
@@ -148,7 +149,7 @@ def tile_rows_conv_res_kernel(tc, x, w0, w1, w2, w3, w4, r, out):
 
         out_rows = out.rearrange("g m n -> m g n")
         for g0, g1, h0, h1 in OUT_BLOCKS:
-            y = sb.tile([M, g1 - g0, (h1 - h0) * HALF], F32, name="y%d_%d" % (g0, h0))
+            y = sb.tile([M, g1 - g0, (h1 - h0) * HALF], F32, name="y%d_%d" % (g0, h0), align_bytes=ALIGN)
             for g in range(g0, g1):
                 for h in range(h0, h1):
                     act = sb.tile([M, HALF], F32, name="act%d_%d" % (g, h))

@@ -24,30 +24,47 @@ BANK = 512
 ALIGN = 256
 
 RUN = 2
-CUT = 768
-ALL, EVEN, ODD = slice(0, 4), slice(0, 4, 2), slice(1, 4, 2)
 V, S = "vector", "scalar"
+X_LOADS = [(0, 512), (512, 768), (768, 1024)]
+EARLY_LOADS = 2
 SHARED = 72
-EARLY = 32
-HELD_FROM = 2
-FIRST_ON_SCALAR = (("x", 1), ALL)
-
-def tail(rows):
-    return [(("x", 6), rows, S, EARLY, WIDTH), (("x", 6), rows, V, 0, EARLY), (("x", 7), rows, V, 0, WIDTH)]
-
+LATE = 64
+FIRST_ON_SCALAR = ("x", 2)
 
 STEPS = [
-    ([(("x", 0), ALL, V, 0, WIDTH), (("x", 1), ALL, S, 0, WIDTH), (("x", 2), ALL, V, 0, WIDTH)], [("x", 0)]),
-    ([(("w", 0), ALL, V, 0, WIDTH), (("x", 3), ALL, S, 0, WIDTH)], [("x", 1), ("x", 2)]),
-    ([(("w", 1), ALL, V, 0, WIDTH), (("x", 4), ALL, S, 0, WIDTH)], [("w", 0), ("x", 3)]),
-    ([(("w", 2), ALL, V, 0, WIDTH), (("x", 5), ALL, S, 0, WIDTH)], [("w", 1), ("x", 4)]),
-    ([(("w", 3), ALL, S, 0, WIDTH)], [("w", 2), ("x", 5)]),
-    ([(("w", 4), ALL, S, SHARED, WIDTH), (("w", 4), ALL, V, 0, SHARED)], [("w", 3), ("w", 4)]),
-    (tail(EVEN) + tail(ODD), [("x", 6), ("x", 7)]),
+    (("x", 0), V, 0, WIDTH),
+    (("x", 2), S, 0, WIDTH),
+    (("x", 1), V, 0, WIDTH),
+    (("x", 3), S, 0, WIDTH),
+    ("x", 0),
+    ("x", 1),
+    ("x", 2),
+    (("x", 4), V, 0, WIDTH),
+    (("x", 5), S, 0, WIDTH),
+    ("x", 3),
+    ("x", 4),
+    (("w", 0), V, 0, WIDTH),
+    ("x", 5),
+    ("w", 0),
+    (("w", 1), V, 0, WIDTH),
+    (("w", 2), S, 0, WIDTH),
+    ("w", 1),
+    (("w", 3), S, SHARED, WIDTH),
+    (("w", 3), V, 0, SHARED),
+    ("w", 2),
+    ("w", 3),
+    (("w", 4), S, SHARED, WIDTH),
+    (("w", 4), V, 0, SHARED),
+    ("w", 4),
+    (("x", 6), S, LATE, WIDTH),
+    (("x", 6), V, 0, LATE),
+    (("x", 7), V, 0, WIDTH),
+    ("x", 6),
+    ("x", 7),
 ]
 
-RESIDUAL_BLOCKS = [(0, 2, 0, 1), (2, 3, 0, 2), (3, 4, 0, 2), (0, 2, 1, 2)]
-OUT_BLOCKS = [(0, 1, 0, 1), (1, 2, 0, 1), (2, 3, 0, 2), (3, 4, 0, 2), (0, 2, 1, 2)]
+RESIDUAL_BLOCKS = [(0, 2, 0, 1), (2, 4, 0, 1), (0, 2, 1, 2), (2, 4, 1, 2)]
+OUT_BLOCKS = [(0, 2, 0, 1), (2, 4, 0, 1), (0, 2, 1, 2), (2, 4, 1, 2)]
 
 
 def tile_rows_conv_res_kernel(tc, x, w0, w1, w2, w3, w4, r, out):
@@ -65,23 +82,20 @@ def tile_rows_conv_res_kernel(tc, x, w0, w1, w2, w3, w4, r, out):
             nc.sync.dma_start(out=tile[:], in_=rows)
             return tile
 
-        x_pairs = x.rearrange("g (p u e) l -> (g p) u (e l)", u=2, e=2)
-        x_runs = sb.tile([P, 2, 2 * L], F32, name="x_runs", align_bytes=ALIGN)
-        nc.sync.dma_start(out=x_runs[:, :, 0 : L + CUT], in_=x_pairs[:, :, 0 : L + CUT])
-        x_early = x_runs[:].rearrange("p u (e l) -> p (u e) l", e=2)
-        w_raw = [
-            load("w_raw%d" % t, w.rearrange("g (p j) m -> (g p) j m", j=PACK)) for t, w in enumerate((w0, w1, w2, w3, w4))
-        ]
-        x_ends = load("x_ends", x_pairs[:, :, L + CUT :])
+        raw = {}
+        x_rows = x.rearrange("g (p j) l -> (g p) j l", j=PACK)
 
-        def raw(piece, rows, first, end):
-            kind, index = piece
-            if kind == "w":
-                return w_raw[index][:, :, first:end]
-            at = index * WIDTH
-            if rows == ODD:
-                return x_ends[:, :, at + first - CUT : at + end - CUT]
-            return x_early[:, rows, at + first : at + end]
+        def load_x(first, end):
+            tile = load("x_raw%d" % first, x_rows[:, :, first:end])
+            for at in range(first, end, WIDTH):
+                raw["x", at // WIDTH] = tile[:, :, at - first : at - first + WIDTH]
+
+        for first, end in X_LOADS[:EARLY_LOADS]:
+            load_x(first, end)
+        for t, w in enumerate((w0, w1, w2, w3, w4)):
+            raw["w", t] = load("w_raw%d" % t, w.rearrange("g (p j) m -> (g p) j m", j=PACK))[:]
+        for first, end in X_LOADS[EARLY_LOADS:]:
+            load_x(first, end)
 
         r_rows = r.rearrange("g m n -> m g n")
         res = {}
@@ -98,12 +112,12 @@ def tile_rows_conv_res_kernel(tc, x, w0, w1, w2, w3, w4, r, out):
 
         grouped, codes, scales = {}, {}, {}
 
-        def interleave(piece, rows, engine, first, end):
+        def interleave(piece, engine, first, end):
             if piece not in grouped:
                 grouped[piece] = sb.tile([P, WIDTH, PACK], BF16, name="grouped_%s%d" % piece, align_bytes=64)
-            source = raw(piece, rows, first, end).rearrange("p j (c i) -> p c j i", i=RUN)
-            target = grouped[piece][:, first:end, rows].rearrange("p (c i) j -> p c j i", i=RUN)
-            if (piece, rows) == FIRST_ON_SCALAR:
+            source = raw[piece][:, :, first:end].rearrange("p j (c i) -> p c j i", i=RUN)
+            target = grouped[piece][:, first:end, :].rearrange("p (c i) j -> p c j i", i=RUN)
+            if piece == FIRST_ON_SCALAR:
                 nc.scalar.activation(out=target, in_=source, func=IDENTITY, bias=bias[:, 0:1])
             elif engine == S:
                 nc.scalar.copy(out=target, in_=source)
@@ -133,17 +147,13 @@ def tile_rows_conv_res_kernel(tc, x, w0, w1, w2, w3, w4, r, out):
                     stop=(t == TAPS - 1 and side == 1),
                 )
 
-        def ready_for(b, t):
-            held = b >= 2 and t >= HELD_FROM and ("w", TAPS - 1) not in codes
-            return ("w", t) in codes and ("x", b + t) in codes and not held
-
         todo = [(b, t) for h in range(2) for t in range(TAPS) for b in (2 * h, 2 * h + 1)]
-        for copies, ready in STEPS:
-            for copy in copies:
-                interleave(*copy)
-            for piece in ready:
-                quantize(piece)
-            for b, t in [(b, t) for b, t in todo if ready_for(b, t)]:
+        for step in STEPS:
+            if len(step) == 4:
+                interleave(*step)
+                continue
+            quantize(step)
+            for b, t in [(b, t) for b, t in todo if ("w", t) in codes and ("x", b + t) in codes]:
                 multiply(b, t)
                 todo.remove((b, t))
 

@@ -25,40 +25,48 @@ ALIGN = 256
 
 RUN = 2
 V, S = "vector", "scalar"
-X_LOADS = [(0, 512), (512, 768), (768, 1024)]
-EARLY_LOADS = 2
+ALL, LOW, HIGH = (0, 4), (0, 2), (2, 4)
+LOADS = [(LOW, 0, 768), (HIGH, 0, 768), 0, 1, 2, 3, 4, (ALL, 768, 1024)]
+X_SPANS = {c: 1 for c in range(8)}
 SHARED = 72
-LATE = 64
-FIRST_ON_SCALAR = ("x", 2)
+LAST = 96
+HELD_FROM = 2
+FIRST_ON_SCALAR = (("x", 4), LOW)
 
 STEPS = [
-    (("x", 0), V, 0, WIDTH),
-    (("x", 2), S, 0, WIDTH),
-    (("x", 1), V, 0, WIDTH),
-    (("x", 3), S, 0, WIDTH),
+    (("x", 0), LOW, V, 0, WIDTH),
+    (("x", 4), LOW, S, 0, WIDTH),
+    (("x", 1), LOW, V, 0, WIDTH),
+    (("x", 5), LOW, S, 0, WIDTH),
+    (("x", 2), LOW, V, 0, WIDTH),
+    (("x", 3), LOW, V, 0, WIDTH),
+    (("x", 0), HIGH, V, 0, WIDTH),
+    (("x", 2), HIGH, S, 0, WIDTH),
+    (("x", 1), HIGH, V, 0, WIDTH),
+    (("x", 3), HIGH, S, 0, WIDTH),
     ("x", 0),
     ("x", 1),
+    (("w", 0), ALL, V, 0, WIDTH),
+    (("x", 4), HIGH, S, 0, WIDTH),
     ("x", 2),
-    (("x", 4), V, 0, WIDTH),
-    (("x", 5), S, 0, WIDTH),
     ("x", 3),
-    ("x", 4),
-    (("w", 0), V, 0, WIDTH),
-    ("x", 5),
     ("w", 0),
-    (("w", 1), V, 0, WIDTH),
-    (("w", 2), S, 0, WIDTH),
+    (("x", 5), HIGH, S, 0, WIDTH),
+    (("w", 1), ALL, V, 0, WIDTH),
+    ("x", 4),
+    ("x", 5),
     ("w", 1),
-    (("w", 3), S, SHARED, WIDTH),
-    (("w", 3), V, 0, SHARED),
+    (("w", 2), ALL, S, 0, WIDTH),
+    (("w", 3), ALL, S, 0, WIDTH),
     ("w", 2),
+    (("w", 4), ALL, S, SHARED, WIDTH),
+    (("w", 4), ALL, V, 0, SHARED),
     ("w", 3),
-    (("w", 4), S, SHARED, WIDTH),
-    (("w", 4), V, 0, SHARED),
     ("w", 4),
-    (("x", 6), S, LATE, WIDTH),
-    (("x", 6), V, 0, LATE),
-    (("x", 7), V, 0, WIDTH),
+    (("x", 6), ALL, S, SHARED, WIDTH),
+    (("x", 6), ALL, V, 0, SHARED),
+    (("x", 7), ALL, S, LAST, WIDTH),
+    (("x", 7), ALL, V, 0, LAST),
     ("x", 6),
     ("x", 7),
 ]
@@ -82,20 +90,27 @@ def tile_rows_conv_res_kernel(tc, x, w0, w1, w2, w3, w4, r, out):
             nc.sync.dma_start(out=tile[:], in_=rows)
             return tile
 
-        raw = {}
         x_rows = x.rearrange("g (p j) l -> (g p) j l", j=PACK)
+        x_raw = {}
 
-        def load_x(first, end):
-            tile = load("x_raw%d" % first, x_rows[:, :, first:end])
-            for at in range(first, end, WIDTH):
-                raw["x", at // WIDTH] = tile[:, :, at - first : at - first + WIDTH]
+        def load_x(rows, first, end):
+            x_raw[rows, first, end] = load("x_raw%d_%d" % (rows[0], first), x_rows[:, rows[0] : rows[1], first:end])
 
-        for first, end in X_LOADS[:EARLY_LOADS]:
-            load_x(first, end)
-        for t, w in enumerate((w0, w1, w2, w3, w4)):
-            raw["w", t] = load("w_raw%d" % t, w.rearrange("g (p j) m -> (g p) j m", j=PACK))[:]
-        for first, end in X_LOADS[EARLY_LOADS:]:
-            load_x(first, end)
+        w_raw = {}
+        for part in LOADS:
+            if isinstance(part, int):
+                w_raw[part] = load("w_raw%d" % part, (w0, w1, w2, w3, w4)[part].rearrange("g (p j) m -> (g p) j m", j=PACK))
+            else:
+                load_x(*part)
+
+        def raw(span, rows, first, end):
+            kind, index = span
+            if kind == "w":
+                return w_raw[index][:, :, first:end]
+            at = index * WIDTH
+            for (held, start, stop), tile in x_raw.items():
+                if held == rows and start <= at + first and at + end <= stop:
+                    return tile[:, :, at + first - start : at + end - start]
 
         r_rows = r.rearrange("g m n -> m g n")
         res = {}
@@ -112,26 +127,31 @@ def tile_rows_conv_res_kernel(tc, x, w0, w1, w2, w3, w4, r, out):
 
         grouped, codes, scales = {}, {}, {}
 
-        def interleave(piece, engine, first, end):
-            if piece not in grouped:
-                grouped[piece] = sb.tile([P, WIDTH, PACK], BF16, name="grouped_%s%d" % piece, align_bytes=64)
-            source = raw[piece][:, :, first:end].rearrange("p j (c i) -> p c j i", i=RUN)
-            target = grouped[piece][:, first:end, :].rearrange("p (c i) j -> p c j i", i=RUN)
-            if piece == FIRST_ON_SCALAR:
+        def pieces(span):
+            return X_SPANS[span[1]] if span[0] == "x" else 1
+
+        def interleave(span, rows, engine, first, end):
+            if span not in grouped:
+                grouped[span] = sb.tile([P, pieces(span) * WIDTH, PACK], BF16, name="grouped_%s%d" % span, align_bytes=64)
+            source = raw(span, rows, first, end).rearrange("p j (c i) -> p c j i", i=RUN)
+            target = grouped[span][:, first:end, rows[0] : rows[1]].rearrange("p (c i) j -> p c j i", i=RUN)
+            if (span, rows) == FIRST_ON_SCALAR:
                 nc.scalar.activation(out=target, in_=source, func=IDENTITY, bias=bias[:, 0:1])
             elif engine == S:
                 nc.scalar.copy(out=target, in_=source)
             else:
                 nc.vector.tensor_copy(out=target, in_=source)
 
-        def quantize(piece):
-            codes[piece] = sb.tile([P, WIDTH], U32, name="codes_%s%d" % piece, align_bytes=64)
-            scales[piece] = sb.tile([P, WIDTH], U8, name="scales_%s%d" % piece, align_bytes=64)
+        def quantize(span):
+            kind, index = span
+            words = sb.tile([P, pieces(span) * WIDTH], U32, name="codes_%s%d" % span, align_bytes=64)
+            plane = sb.tile([P, pieces(span) * WIDTH], U8, name="scales_%s%d" % span, align_bytes=64)
             nc.vector.quantize_mx(
-                out=codes[piece][:].bitcast(FP8X4),
-                scales=scales[piece][:],
-                in_=grouped[piece][:].rearrange("p c j -> p (c j)"),
+                out=words[:].bitcast(FP8X4), scales=plane[:], in_=grouped[span][:].rearrange("p c j -> p (c j)")
             )
+            for i in range(pieces(span)):
+                codes[kind, index + i] = words[:, i * WIDTH : (i + 1) * WIDTH]
+                scales[kind, index + i] = plane[:, i * WIDTH : (i + 1) * WIDTH]
 
         def multiply(b, t):
             side = b % 2
@@ -147,13 +167,17 @@ def tile_rows_conv_res_kernel(tc, x, w0, w1, w2, w3, w4, r, out):
                     stop=(t == TAPS - 1 and side == 1),
                 )
 
+        def ready_for(b, t):
+            held = b >= 2 and t >= HELD_FROM and ("w", TAPS - 1) not in codes
+            return ("w", t) in codes and ("x", b + t) in codes and not held
+
         todo = [(b, t) for h in range(2) for t in range(TAPS) for b in (2 * h, 2 * h + 1)]
         for step in STEPS:
-            if len(step) == 4:
+            if len(step) == 5:
                 interleave(*step)
                 continue
             quantize(step)
-            for b, t in [(b, t) for b, t in todo if ("w", t) in codes and ("x", b + t) in codes]:
+            for b, t in [(b, t) for b, t in todo if ready_for(b, t)]:
                 multiply(b, t)
                 todo.remove((b, t))
 

@@ -26,37 +26,25 @@ ALIGN = 256
 RUN = 2
 V, S = "vector", "scalar"
 ALL, LOW, HIGH = (0, 4), (0, 2), (2, 4)
-LOADS = [(LOW, 0, 768), (HIGH, 0, 768), 0, 1, 2, 3, 4, (ALL, 768, 1024)]
-X_SPANS = {c: 1 for c in range(8)}
+LOADS = [(ALL, 0, 768), 0, 1, 2, 3, 4, (ALL, 768, 896), (ALL, 896, 1024)]
+X_SPANS = {0: 2, 2: 2, 4: 2, 6: 1, 7: 1}
 SHARED = 72
 LAST = 96
 HELD_FROM = 2
-FIRST_ON_SCALAR = (("x", 4), LOW)
+FIRST_ON_SCALAR = (("x", 2), ALL)
 
 STEPS = [
-    (("x", 0), LOW, V, 0, WIDTH),
-    (("x", 4), LOW, S, 0, WIDTH),
-    (("x", 1), LOW, V, 0, WIDTH),
-    (("x", 5), LOW, S, 0, WIDTH),
-    (("x", 2), LOW, V, 0, WIDTH),
-    (("x", 3), LOW, V, 0, WIDTH),
-    (("x", 0), HIGH, V, 0, WIDTH),
-    (("x", 2), HIGH, S, 0, WIDTH),
-    (("x", 1), HIGH, V, 0, WIDTH),
-    (("x", 3), HIGH, S, 0, WIDTH),
-    ("x", 0),
-    ("x", 1),
+    (("x", 0), ALL, V, 0, 2 * WIDTH),
+    (("x", 2), ALL, S, 0, 2 * WIDTH),
     (("w", 0), ALL, V, 0, WIDTH),
-    (("x", 4), HIGH, S, 0, WIDTH),
-    ("x", 2),
-    ("x", 3),
+    ("x", 0),
     ("w", 0),
-    (("x", 5), HIGH, S, 0, WIDTH),
     (("w", 1), ALL, V, 0, WIDTH),
-    ("x", 4),
-    ("x", 5),
+    (("x", 4), ALL, S, 0, 2 * WIDTH),
+    ("x", 2),
     ("w", 1),
-    (("w", 2), ALL, S, 0, WIDTH),
+    (("w", 2), ALL, V, 0, WIDTH),
+    ("x", 4),
     (("w", 3), ALL, S, 0, WIDTH),
     ("w", 2),
     (("w", 4), ALL, S, SHARED, WIDTH),

@@ -26,7 +26,7 @@ ALIGN = 256
 RUN = 2
 V, S = "vector", "scalar"
 ALL, LOW, HIGH = (0, 4), (0, 2), (2, 4)
-LOADS = [(ALL, 0, 768), 0, 1, 2, 3, 4, (ALL, 768, 896), (ALL, 896, 1024)]
+LOADS = [(ALL, 0, 768), 0, 1, 2, 3, 4, (ALL, 768, 1024)]
 X_SPANS = {0: 2, 2: 2, 4: 2, 6: 1, 7: 1}
 SHARED = 72
 LAST = 96
@@ -59,8 +59,8 @@ STEPS = [
     ("x", 7),
 ]
 
-RESIDUAL_BLOCKS = [(0, 2, 0, 1), (2, 4, 0, 1), (0, 2, 1, 2), (2, 4, 1, 2)]
-OUT_BLOCKS = [(0, 2, 0, 1), (2, 4, 0, 1), (0, 2, 1, 2), (2, 4, 1, 2)]
+RESIDUAL_BLOCKS = [(0, 2, 0, 1), (2, 3, 0, 2), (3, 4, 0, 2), (0, 2, 1, 2)]
+OUT_BLOCKS = [(0, 2, 0, 1), (2, 3, 0, 2), (3, 4, 0, 2), (0, 2, 1, 2)]
 
 
 def tile_rows_conv_res_kernel(tc, x, w0, w1, w2, w3, w4, r, out):

@@ -26,10 +26,10 @@ ALIGN = 256
 RUN = 2
 V, S = "vector", "scalar"
 ALL, LOW, HIGH = (0, 4), (0, 2), (2, 4)
-LOADS = [(ALL, 0, 768), 0, 1, 2, 3, 4, (ALL, 768, 1024)]
+LOADS = [(ALL, 0, 768), 0, 1, 2, 3, 4, (LOW, 768, 1024), (HIGH, 768, 1024)]
 X_SPANS = {0: 2, 2: 2, 4: 2, 6: 1, 7: 1}
 SHARED = 72
-LAST = 96
+LAST = 64
 HELD_FROM = 2
 FIRST_ON_SCALAR = (("x", 2), ALL)
 
@@ -51,10 +51,11 @@ STEPS = [
     (("w", 4), ALL, V, 0, SHARED),
     ("w", 3),
     ("w", 4),
-    (("x", 6), ALL, S, SHARED, WIDTH),
-    (("x", 6), ALL, V, 0, SHARED),
-    (("x", 7), ALL, S, LAST, WIDTH),
-    (("x", 7), ALL, V, 0, LAST),
+    (("x", 6), LOW, S, 0, WIDTH),
+    (("x", 7), LOW, V, 0, WIDTH),
+    (("x", 6), HIGH, S, LAST, WIDTH),
+    (("x", 6), HIGH, V, 0, LAST),
+    (("x", 7), HIGH, V, 0, WIDTH),
     ("x", 6),
     ("x", 7),
 ]

from contextlib import ExitStack

import concourse.mybir as mybir

G, D, M, N, L = 4, 128, 128, 512, 1024
TAPS = 5
WIDTH = 128
CHUNKS = N // WIDTH
HALF = N // 2
FLOPS = 2 * G * TAPS * D * M * N

F32 = mybir.dt.float32
BF16 = mybir.dt.bfloat16
U32 = mybir.dt.uint32
U8 = mybir.dt.uint8
FP8X4 = mybir.dt.float8_e4m3fn_x4
GELU = mybir.ActivationFunctionType.Gelu_apprx_tanh
IDENTITY = mybir.ActivationFunctionType.Identity

P = 128
PACK = 4
ROWS = D // PACK
BANK = 512
ALIGN = 256

RUN = 2
V, S = "vector", "scalar"
ALL, LOW, HIGH = (0, 4), (0, 2), (2, 4)
LOADS = [(ALL, 0, 768), 0, 1, 2, 3, 4, (LOW, 768, 1024), (HIGH, 768, 1024)]
X_SPANS = {0: 2, 2: 2, 4: 2, 6: 1, 7: 1}
SHARED = 72
LAST = 64
HELD_FROM = 2
FIRST_ON_SCALAR = (("x", 2), ALL)

STEPS = [
    (("x", 0), ALL, V, 0, 2 * WIDTH),
    (("x", 2), ALL, S, 0, 2 * WIDTH),
    (("w", 0), ALL, V, 0, WIDTH),
    ("x", 0),
    ("w", 0),
    (("w", 1), ALL, V, 0, WIDTH),
    (("x", 4), ALL, S, 0, 2 * WIDTH),
    ("x", 2),
    ("w", 1),
    (("w", 2), ALL, V, 0, WIDTH),
    ("x", 4),
    (("w", 3), ALL, S, 0, WIDTH),
    ("w", 2),
    (("w", 4), ALL, S, SHARED, WIDTH),
    (("w", 4), ALL, V, 0, SHARED),
    ("w", 3),
    ("w", 4),
    (("x", 6), LOW, S, 0, WIDTH),
    (("x", 7), LOW, V, 0, WIDTH),
    (("x", 6), HIGH, S, LAST, WIDTH),
    (("x", 6), HIGH, V, 0, LAST),
    (("x", 7), HIGH, V, 0, WIDTH),
    ("x", 6),
    ("x", 7),
]

RESIDUAL_BLOCKS = [(0, 2, 0, 1), (2, 3, 0, 2), (3, 4, 0, 2), (0, 2, 1, 2)]
OUT_BLOCKS = [(0, 2, 0, 1), (2, 3, 0, 2), (3, 4, 0, 2), (0, 2, 1, 2)]


def tile_rows_conv_res_kernel(tc, x, w0, w1, w2, w3, w4, r, out):
    nc = tc.nc

    with ExitStack() as ctx:
        sb = ctx.enter_context(tc.tile_pool(name="sb", bufs=1))
        psum = ctx.enter_context(tc.psum_pool(name="psum", bufs=1))
        ctx.enter_context(tc.manual_schedule())

        banks = [[psum.tile([M, BANK], F32, name="bank%d_%d" % (g, h)) for h in range(2)] for g in range(G)]

        def load(name, rows):
            tile = sb.tile(list(rows.shape), F32, name=name, align_bytes=ALIGN)
            nc.sync.dma_start(out=tile[:], in_=rows)
            return tile

        x_rows = x.rearrange("g (p j) l -> (g p) j l", j=PACK)
        x_raw = {}

        def load_x(rows, first, end):
            x_raw[rows, first, end] = load("x_raw%d_%d" % (rows[0], first), x_rows[:, rows[0] : rows[1], first:end])

        w_raw = {}
        for part in LOADS:
            if isinstance(part, int):
                w_raw[part] = load("w_raw%d" % part, (w0, w1, w2, w3, w4)[part].rearrange("g (p j) m -> (g p) j m", j=PACK))
            else:
                load_x(*part)

        def raw(span, rows, first, end):
            kind, index = span
            if kind == "w":
                return w_raw[index][:, :, first:end]
            at = index * WIDTH
            for (held, start, stop), tile in x_raw.items():
                if held == rows and start <= at + first and at + end <= stop:
                    return tile[:, :, at + first - start : at + end - start]

        r_rows = r.rearrange("g m n -> m g n")
        res = {}
        for g0, g1, h0, h1 in RESIDUAL_BLOCKS:
            tile = load("res%d_%d" % (g0, h0), r_rows[:, g0:g1, h0 * HALF : h1 * HALF])
            for g in range(g0, g1):
                for h in range(h0, h1):
                    res[g, h] = tile[:, g - g0, (h - h0) * HALF : (h - h0 + 1) * HALF]

        zero = sb.tile([P, 8], F32, name="zero")
        bias = sb.tile([P, 8], F32, name="bias")
        nc.vector.memset(zero[:], 0.0)
        nc.scalar.activation(out=bias[:], in_=zero[:], func=GELU)

        grouped, codes, scales = {}, {}, {}

        def pieces(span):
            return X_SPANS[span[1]] if span[0] == "x" else 1

        def interleave(span, rows, engine, first, end):
            if span not in grouped:
                grouped[span] = sb.tile([P, pieces(span) * WIDTH, PACK], BF16, name="grouped_%s%d" % span, align_bytes=64)
            source = raw(span, rows, first, end).rearrange("p j (c i) -> p c j i", i=RUN)
            target = grouped[span][:, first:end, rows[0] : rows[1]].rearrange("p (c i) j -> p c j i", i=RUN)
            if (span, rows) == FIRST_ON_SCALAR:
                nc.scalar.activation(out=target, in_=source, func=IDENTITY, bias=bias[:, 0:1])
            elif engine == S:
                nc.scalar.copy(out=target, in_=source)
            else:
                nc.vector.tensor_copy(out=target, in_=source)

        def quantize(span):
            kind, index = span
            words = sb.tile([P, pieces(span) * WIDTH], U32, name="codes_%s%d" % span, align_bytes=64)
            plane = sb.tile([P, pieces(span) * WIDTH], U8, name="scales_%s%d" % span, align_bytes=64)
            nc.vector.quantize_mx(
                out=words[:].bitcast(FP8X4), scales=plane[:], in_=grouped[span][:].rearrange("p c j -> p (c j)")
            )
            for i in range(pieces(span)):
                codes[kind, index + i] = words[:, i * WIDTH : (i + 1) * WIDTH]
                scales[kind, index + i] = plane[:, i * WIDTH : (i + 1) * WIDTH]

        def multiply(b, t):
            side = b % 2
            for g in range(G):
                part = slice(g * ROWS, (g + 1) * ROWS)
                nc.tensor.matmul_mx(
                    out=banks[g][b // 2][:, side * WIDTH : (side + 1) * WIDTH],
                    lhsT=codes["w", t][part, :].bitcast(FP8X4),
                    lhsT_scale=scales["w", t][part, :],
                    rhs=codes["x", b + t][part, :].bitcast(FP8X4),
                    rhs_scale=scales["x", b + t][part, :],
                    start=(t == 0 and side == 0),
                    stop=(t == TAPS - 1 and side == 1),
                )

        def ready_for(b, t):
            held = b >= 2 and t >= HELD_FROM and ("w", TAPS - 1) not in codes
            return ("w", t) in codes and ("x", b + t) in codes and not held

        todo = [(b, t) for h in range(2) for t in range(TAPS) for b in (2 * h, 2 * h + 1)]
        for step in STEPS:
            if len(step) == 5:
                interleave(*step)
                continue
            quantize(step)
            for b, t in [(b, t) for b, t in todo if ready_for(b, t)]:
                multiply(b, t)
                todo.remove((b, t))

        out_rows = out.rearrange("g m n -> m g n")
        for g0, g1, h0, h1 in OUT_BLOCKS:
            y = sb.tile([M, g1 - g0, (h1 - h0) * HALF], F32, name="y%d_%d" % (g0, h0), align_bytes=ALIGN)
            for g in range(g0, g1):
                for h in range(h0, h1):
                    act = sb.tile([M, HALF], F32, name="act%d_%d" % (g, h))
                    nc.scalar.activation(out=act[:], in_=banks[g][h][:, 0:HALF], func=GELU)
                    cols = slice((h - h0) * HALF, (h - h0 + 1) * HALF)
                    nc.vector.tensor_add(out=y[:, g - g0, cols], in0=act[:], in1=res[g, h])
            nc.sync.dma_start(out=out_rows[:, g0:g1, h0 * HALF : h1 * HALF], in_=y[:])
